import numpy as np, ml_dtypes
CORES = [8,9,10,11,12,13]
N = 6
import mx_ref
BF = ml_dtypes.bfloat16
def entries(a):
    return np.ascontiguousarray(a.T).reshape(-1)
def table(e):
    return np.ascontiguousarray(np.reshape(e, (-1, 16)).T).astype(np.int32)
def gentries(a):
    return np.ascontiguousarray(a.reshape(8, 16, -1).transpose(0, 2, 1)).reshape(8, -1)
def gtable(e):
    e = np.asarray(e); return np.ascontiguousarray(e.reshape(8, -1, 16).transpose(0, 2, 1)).reshape(128, -1).astype(np.int32)
def tile(rs):
    return np.stack(rs, axis=2).reshape(128, -1).astype(BF)
def cut(t, i, w=512):
    return t[:, w * i:w * i + w]
def f(rng, *shape):
    return mx_ref.flush((rng.standard_normal(shape, dtype=np.float32) * np.exp2(rng.integers(-2, 3, shape[:-1] + (1,)))).astype(BF))
def wide(rng, *shape, cols=0):
    v = rng.standard_normal(shape, dtype=np.float32) * np.exp2(rng.integers(-12, 13, shape)).astype(np.float32)
    if cols: v *= np.repeat(np.exp2(rng.integers(-cols, cols + 1, shape[:-2] + (1, shape[-1] // 4))) * (rng.random(shape[:-2] + (1, shape[-1] // 4)) > 0.0625), 4, axis=-1).astype(np.float32)
    return mx_ref.flush(v.astype(BF))
T, CAPP, P = 512, 64, 256
SL = N * CAPP
G = 8
def pieces(rng, how):
    if how == "ones": n = np.ones((G, SL), int)
    elif how == "full":
        n = T - rng.integers(0, 8, (G, SL)); n[:, ::4] = T
    elif how == "powers":
        k = [1 << i for i in range(T.bit_length())]; k = sorted(set(k + [i + 1 for i in k if i < T]))
        n = rng.permuted(np.tile(np.resize(k, SL), (G, 1)), axis=1)
    else: n = np.where(rng.random((G, SL)) < 0.5, rng.integers(1, T + 1, (G, SL)), np.clip(np.exp2(rng.uniform(0, T.bit_length() - 1, (G, SL))).astype(int), 1, T))
    s = rng.integers(0, T - n + 1)
    if how == "full": s[:] = 0
    if how == "nested":
        for g in range(G):
            for r in range(N):
                m = rng.integers(0, T)
                b = np.sort(rng.choice(rng.integers(0, m + 1, 16), CAPP)); e = np.sort(rng.choice(rng.integers(m, T, 16), CAPP))[::-1]
                k = r * CAPP + rng.permutation(CAPP); s[g, k] = b; n[g, k] = e - b + 1
    return s, n
def lists(rng, how="any", every=False):
    held = np.zeros((N, N, CAPP), bool)
    for r in range(N):
        n = rng.integers(0, CAPP + 1, N); n[(r + rng.integers(1, N)) % N] = CAPP
        for q in range(N): held[q, r, rng.permutation(CAPP)[:CAPP if every else n[q]]] = True
    d = {"lo": [], "ln": [], "pf": [], "pg": []}
    for q in range(N):
        s, n = pieces(rng, how); e = ~held[q].reshape(-1)
        s[:, e] = -1; n[:, e] = 0
        d["lo"].append(gtable(s)); d["ln"].append(gtable(n))
    who = rng.permutation(N)
    for r in range(N):
        k = rng.permutation(np.flatnonzero(held[:, r]))
        first = rng.permutation(np.resize(k, P))
        second = np.where(rng.random(P) < 0.25, -1, rng.choice(k, P))
        if how == "ones":
            if r == who[0]:
                first[rng.permutation(P)[:P // 2]] = k[0]; second[rng.permutation(P)[:P // 2]] = k[0]
            if r == who[1]: second[:] = -1
            if r == who[2]: second = rng.choice(k, P)
        d["pf"].append(table(first))
        d["pg"].append(table(second))
    return {k: np.stack(t) for k, t in d.items()}
def setup_inputs(rng):
    return {"x": f(rng, N, 128, 4 * T), "a": f(rng, N, 128, 2048), "u": f(rng, N, 128, 512), "v": f(rng, N, 128, 512), **lists(rng)}
def setup_inputs_ones(rng):
    return {**setup_inputs(rng), **lists(rng, "ones")}
def setup_inputs_full(rng):
    return {**setup_inputs(rng), **lists(rng, "full", True)}
def setup_inputs_powers(rng):
    return {**setup_inputs(rng), **lists(rng, "powers", True)}
def setup_inputs_nested(rng):
    return {**setup_inputs(rng), **lists(rng, "nested", True)}
def setup_inputs_spread(rng):
    d = setup_inputs(rng); d["x"] = wide(rng, N, 128, 4 * T, cols=8); return d
def check_inputs(d):
    b = []; held = []
    for q in range(N):
        s, n = gentries(d["lo"][q]).reshape(G, -1), gentries(d["ln"][q]).reshape(G, -1)
        e = s == -1; held.append(~e[0])
        if s.min() < -1 or s.max() >= T or (e != e[:1]).any(): b.append("lo")
        if (n[e] != 0).any() or (n[~e] < 1).any() or (n[~e] > T - s[~e]).any(): b.append("ln")
    for r in range(N):
        h = np.concatenate([held[q][r * CAPP:r * CAPP + CAPP] for q in range(N)])
        for k, least in (("pf", 0), ("pg", -1)):
            j = entries(d[k][r])
            if j.min() < least or j.max() >= SL or not h[j[(j >= 0) & (j < SL)]].all(): b.append(k)
    return b
def reference(x, a, u, v, lo, ln, pf, pg):
    sent = []
    for q in range(N):
        X = mx_ref.quantize(x[q])
        Z = np.stack([mx_ref.matmul(mx_ref.quantize(np.ascontiguousarray(cut(a[q], i))), X) for i in range(4)])
        h = np.maximum(Z, np.float32(0)) * np.float32(0.05)
        s, n = gentries(lo[q]), gentries(ln[q])
        R = np.zeros((4, 128, SL), np.float32)
        for k in range(SL):
            for g in range(8):
                if n[g, k]: R[:, 16 * g:16 * g + 16, k] = h[:, 16 * g:16 * g + 16, s[g, k]:s[g, k] + n[g, k]].max(axis=2)
        sent.append([mx_ref.quantize(np.ascontiguousarray(tile([R[i][:, CAPP * r:CAPP * r + CAPP] for i in range(4)]))) for r in range(N)])
    y = np.zeros((N, 128, P), np.float32)
    for r in range(N):
        V, U = mx_ref.quantize(v[r]), mx_ref.quantize(u[r])
        zv = np.concatenate([mx_ref.matmul(V, sent[q][r]) for q in range(N)], axis=1)
        zu = np.concatenate([mx_ref.matmul(U, sent[q][r]) for q in range(N)], axis=1)
        first, second = entries(pf[r]), entries(pg[r])
        y[r] = zv[:, first]
        two = second >= 0
        y[r][:, two] += zu[:, second[two]]
    return {"y": y}

@@ -1,0 +1,328 @@
+from concourse.bass import DstId, RemoteDMATransfer
+from concourse.mybir import dt, AluOpType, ActivationFunctionType
+
+N, T_COLS, CAPP, P = 6, 512, 64, 256
+SL = N * CAPP
+NS = SL // 16
+HALF = SL // 2
+H0 = 128
+EX = 640
+S4 = EX + 7 * 256
+P4 = S4 + 512
+WS = 3584
+
+SCRATCH = {
+    "xb": ("sbuf", [128, 2048], "bfloat16"), "ab": ("sbuf", [128, 2048], "bfloat16"),
+    "ub": ("sbuf", [128, 512], "bfloat16"), "vb": ("sbuf", [128, 512], "bfloat16"),
+    "xq": ("sbuf", [128, 512], "float8_e4m3fn_x4"), "xs": ("sbuf", [128, 512], "uint8"),
+    "aq": ("sbuf", [128, 512], "float8_e4m3fn_x4"), "sa": ("sbuf", [128, 512], "uint8"),
+    "uq": ("sbuf", [128, 128], "float8_e4m3fn_x4"), "us": ("sbuf", [128, 128], "uint8"),
+    "vq": ("sbuf", [128, 128], "float8_e4m3fn_x4"), "vs": ("sbuf", [128, 128], "uint8"),
+    "cq": ("sbuf", [128, SL], "float8_e4m3fn_x4"), "cs": ("sbuf", [128, SL], "uint8"),
+    "rq": ("sbuf", [128, 320], "float8_e4m3fn_x4"), "rs": ("sbuf", [128, 320], "uint8"),
+    "win": ("sbuf", [128, 4 * WS], "bfloat16"),
+    "tile": ("sbuf", [128, 4 * SL], "bfloat16"),
+    "ones": ("sbuf", [128, 1152], "bfloat16"), "m3": ("sbuf", [128, 1152], "bfloat16"),
+    "m2": ("sbuf", [128, 384], "bfloat16"), "m4": ("sbuf", [128, 512], "bfloat16"),
+    "mc": ("sbuf", [128, 6 * 128], "bfloat16"), "m7": ("sbuf", [128, 7 * NS], "bfloat16"),
+    "lr": ("sbuf", [128, 2 * NS], "int32"), "ln_": ("sbuf", [128, NS], "int32"), "lm": ("sbuf", [128, NS], "int32"),
+    "sh": ("sbuf", [128, 14 * NS], "int32"), "fl": ("sbuf", [128, 7 * NS], "bfloat16"),
+    "cn": ("sbuf", [128, 7 * NS], "bfloat16"), "ee": ("sbuf", [128, 2 * NS], "float32"),
+    "yy": ("sbuf", [128, 2 * NS], "float32"), "pm": ("sbuf", [128, NS], "float32"),
+    "xm": ("sbuf", [128, 2 * NS], "float32"), "of": ("sbuf", [128, 4 * NS], "float32"),
+    "ou": ("sbuf", [128, 4 * NS], "uint16"),
+    "pl": ("sbuf", [128, 32], "int32"), "pa": ("sbuf", [128, 32], "int32"), "pb": ("sbuf", [128, 32], "int32"),
+    "pc": ("sbuf", [128, 32], "int32"), "pz": ("sbuf", [128, 16], "int32"), "pu": ("sbuf", [128, 32], "uint16"),
+    "zu": ("sbuf", [128, 400], "float32"), "zv": ("sbuf", [128, 384], "float32"),
+    "gu": ("sbuf", [128, P], "float32"), "yb": ("sbuf", [128, P], "float32"),
+    "zp": ("psum", [128, 2048], "float32"), "pp": ("psum", [128, 2048], "float32"),
+}
+for _k in ("00", "10", "20", "21", "30", "31"):
+    _n = 3 * (SL if _k in ("00", "10") else HALF)
+    SCRATCH["g" + _k] = ("sbuf", [128, _n], "bfloat16")
+    SCRATCH["s" + _k] = ("sbuf", [128, _n], "bfloat16")
+SEMAPHORES = ["cv", "cs_", "ct", "cg", "lists", "x0", "x1", "a0", "a1", "a2", "uv", "pfg", "y0", "y1", "arr", "sent"]
+
+
+def slot_order(q, T, topo):
+    me = T.cores[q]
+    rest = [(q + d) % N for d in range(1, N)]
+    far = sorted(r for r in rest if topo.die(T.cores[r]) != topo.die(me))
+    near = [r for r in rest if topo.die(T.cores[r]) == topo.die(me)]
+    return far + near + [q]
+
+
+def runs(order):
+    out = []
+    for k, r in enumerate(order):
+        if out and out[-1][1] + out[-1][2] == r:
+            out[-1][2] += 1
+        else:
+            out.append([k, r, 1])
+    return out
+
+
+def sending(q, T, topo):
+    order = slot_order(q, T, topo)
+    eng = topo.engines(T.cores[q], T.cores[order[0]])
+    ev, od = eng[0::2], eng[1::2]
+    k = len(ev) // 2
+    first = [ev[:k], ev[k:], od], [od[:k], od[k:], ev]
+    last = [ev, od], [od, ev]
+    return [[(j, order[j], e) for j, e in enumerate(es)] for es in first], [[(3 + j, order[3 + j], e) for j, e in enumerate(es)] for es in last]
+
+
+def rank_program(g, core, T, topo):
+    rank = T.rank_of(core)
+    if rank is None:
+        return
+    A, F = AluOpType, ActivationFunctionType
+    que = {"cv": g.vector, "cs_": g.scalar, "ct": g.tensor, "cg": g, "sy": g.sync}
+    count = {k: 0 for k in que}
+    seen = {k: {} for k in que}
+    v, s, t = g.vector, g.scalar, g.tensor
+
+    def need(q, *toks):
+        for sem, val in toks:
+            if seen[q].get(sem, 0) < val:
+                que[q].wait_ge(T.sem[sem], val)
+                seen[q][sem] = val
+
+    def done(q, ins):
+        ins.then_inc(T.sem[q], 1)
+        count[q] += 1
+        return (q, count[q])
+
+    order = slot_order(rank, T, topo)
+    rn = runs(order)
+
+    for k, r, n in rn:
+        s.dma_start(T.ln_[:, 4 * k:4 * (k + n)], T.ln[:, 4 * r:4 * (r + n)]).then_inc(T.sem.lists, 16)
+        s.dma_start(T.lr[:, 4 * k:4 * (k + n)], T.lo[:, 4 * r:4 * (r + n)]).then_inc(T.sem.lists, 16)
+    L_LISTS = ("lists", 32 * len(rn))
+    g.sync.dma_start(T.xb[:, 0:1024], T.x[:, 0:1024]).then_inc(T.sem.x0, 16)
+    g.sync.dma_start(T.ab[:, 0:512], T.a[:, 0:512]).then_inc(T.sem.a0, 16)
+    g.sync.dma_start(T.xb[:, 1024:2048], T.x[:, 1024:2048]).then_inc(T.sem.x1, 16)
+    g.sync.dma_start(T.ab[:, 512:1024], T.a[:, 512:1024]).then_inc(T.sem.a1, 16)
+    g.sync.dma_start(T.ab[:, 1024:2048], T.a[:, 1024:2048]).then_inc(T.sem.a2, 16)
+    g.sync.dma_start(T.ub[:], T.u[:]).then_inc(T.sem.uv, 16)
+    g.sync.dma_start(T.vb[:], T.v[:]).then_inc(T.sem.uv, 16)
+    for k in range(8):
+        g.sync.dma_start(T.pl[16 * k:16 * k + 16, 0:16], T.pf[:]).then_inc(T.sem.pfg, 16)
+        g.sync.dma_start(T.pl[16 * k:16 * k + 16, 16:32], T.pg[:]).then_inc(T.sem.pfg, 16)
+
+    k_one = done("cv", v.memset(T.ones[:], 1.0))
+    k_m7 = done("cv", v.memset(T.m7[:], 1.0))
+    for i in range(4):
+        done("cv", v.memset(T.win[:, i * WS:i * WS + H0], 0.0))
+        done("cv", v.memset(T.win[:, i * WS + EX:i * WS + EX + 256], 0.0))
+    need("cv", k_m7)
+    done("cv", v.memset(T.m7[:, 0::7], 0.0))
+    k_m7 = done("cv", v.memset(T.m7[:, 1::7], 2.5))
+    k_z = ("cv", count["cv"] - 2)
+    need("cv", k_z)
+    done("cv", v.memset(T.win[:, 128::256], 0.0))
+    k_win = done("cv", v.memset(T.win[:, 127::256], 0.0))
+    k_zu = done("cv", v.memset(T.zu[:, 384:400], 0.0))
+
+    need("cg", k_one)
+
+    def mask(out, n, b):
+        return done("cg", g.affine_select(out, T.ones[:, 0:n], [[0, n // b], [1, b]], A.is_gt, 0.0, 0, 0))
+
+    k_m4 = mask(T.m4[:], 512, 4)
+    for m in range(1, 7):
+        k_mc = mask(T.mc[:, 128 * (m - 1):128 * m], 128, 1 << m)
+    k_m3 = mask(T.m3[:], 1152, 3)
+    k_m2 = mask(T.m2[:], 384, 2)
+
+    need("cv", L_LISTS)
+    k = done("cv", v.tensor_scalar(T.lm[:], T.ln_[:], -1, None, A.add))
+    done("cv", v.tensor_scalar(T.ee[:, 0:NS], T.ln_[:], 2, -1, A.min, A.add))
+    k_ee = done("cv", v.tensor_scalar(T.ee[:, NS:2 * NS], T.ln_[:], 2, -(1 + H0), A.min, A.add))
+    need("cv", k)
+    k_lr = done("cv", v.tensor_tensor(T.lr[:, NS:2 * NS], T.lr[:, 0:NS], T.lm[:], A.add))
+    need("cv", k_lr)
+    for j in range(7):
+        k_sh = done("cv", v.tensor_scalar(T.sh[:, j::7], T.lr[:], 2 + j, None, A.arith_shift_right))
+    done("cv", v.tensor_tensor(T.yy[:, 0:NS], T.lr[:, 0:NS], T.ee[:, 0:NS], A.add))
+    k_yy = done("cv", v.tensor_tensor(T.yy[:, NS:2 * NS], T.lr[:, NS:2 * NS], T.ee[:, NS:2 * NS], A.subtract))
+    need("cv", k_sh)
+    k_fl = done("cv", v.tensor_tensor(T.fl[:], T.sh[:, 0:7 * NS], T.sh[:, 7 * NS:14 * NS], A.not_equal))
+
+    def quant(out, sc, src, *deps):
+        need("cv", *deps)
+        return done("cv", v.quantize_mx(out, sc, src))
+
+    k_x0 = quant(T.xq[:, 0:256], T.xs[:, 0:256], T.xb[:, 0:1024], ("x0", 16))
+    k_a = [quant(T.aq[:, 0:128], T.sa[:, 0:128], T.ab[:, 0:512], ("a0", 16))]
+    k_x1 = quant(T.xq[:, 256:512], T.xs[:, 256:512], T.xb[:, 1024:2048], ("x1", 16))
+
+    need("cv", k_fl)
+    k_cn = done("cv", v.tensor_tensor_scan(T.cn[:], T.m7[:], T.fl[:], 0.0, A.mult, A.add))
+    done("cv", v.tensor_scalar(T.of[:, 0:NS], T.fl[:, 0::7], S4 - H0, None, A.mult))
+    k_of = done("cv", v.tensor_scalar(T.of[:, NS:2 * NS], T.fl[:, 0::7], P4 - H0, None, A.mult))
+    k_a.append(quant(T.aq[:, 128:256], T.sa[:, 128:256], T.ab[:, 512:1024], ("a1", 16)))
+    need("cv", k_cn)
+    k_pm = done("cv", v.tensor_scalar(T.pm[:], T.cn[:, 6::7], 256, None, A.mult))
+    need("cv", k_of)
+    done("cv", v.tensor_tensor(T.of[:, 0:2 * NS], T.of[:, 0:2 * NS], T.lr[:], A.add))
+    need("cv", k_pm)
+    done("cv", v.tensor_tensor(T.xm[:, 0:NS], T.sh[:, 0:7 * NS:7], T.pm[:], A.add))
+    k_xm = done("cv", v.tensor_tensor(T.xm[:, NS:2 * NS], T.sh[:, 7 * NS:14 * NS:7], T.pm[:], A.add))
+    k_a.append(quant(T.aq[:, 256:512], T.sa[:, 256:512], T.ab[:, 1024:2048], ("a2", 16)))
+    k_a.append(k_a[2])
+    need("cv", k_xm)
+    k = done("cv", v.tensor_tensor(T.of[:, 2 * NS:4 * NS], T.xm[:], T.yy[:], A.max))
+    need("cv", k)
+    k_ou = done("cv", v.tensor_copy(T.ou[:], T.of[:]))
+
+    def mm(out, w, ws, x, xs, *deps):
+        need("ct", *deps)
+        return done("ct", t.matmul_mx(out, w, ws, x, xs, True, True))
+
+    def relu(i, c, n, src, *deps):
+        need("cs_", *deps)
+        b = i * WS + H0 + c
+        return done("cs_", s.activation(T.win[:, b:b + n], src, F.Relu, scale=0.05))
+
+    k0 = mm(T.zp[:, 0:256], T.aq[:, 0:128], T.sa[:, 0:128], T.xq[:, 0:256], T.xs[:, 0:256], k_a[0])
+    k1 = mm(T.pp[:, 1536:1792], T.aq[:, 0:128], T.sa[:, 0:128], T.xq[:, 256:512], T.xs[:, 256:512], k_x1)
+    k_h = [[relu(0, 0, 256, T.zp[:, 0:256], k_win, k0), relu(0, 256, 256, T.pp[:, 1536:1792], k1)]]
+    for i in (1, 2, 3):
+        kk = mm(T.zp[:, 512 * i:512 * i + 512], T.aq[:, 128 * i:128 * i + 128], T.sa[:, 128 * i:128 * i + 128], T.xq[:], T.xs[:], k_a[i])
+        k_h.append([relu(i, 0, 512, T.zp[:, 512 * i:512 * i + 512], kk)])
+
+    def tables(i):
+        w = i * WS
+        need("cv", k_m4)
+        step = T_COLS // len(k_h[i])
+        for c, kh in enumerate(k_h[i]):
+            need("cv", kh)
+            a, b = c * step, (c + 1) * step
+            k_p = done("cv", v.tensor_tensor_scan(T.win[:, w + P4 + a:w + P4 + b], T.m4[:, a:b], T.win[:, w + H0 + a:w + H0 + b], 0.0, A.mult, A.max))
+        done("cv", v.tensor_tensor_scan(T.win[:, w + S4 + 511:w + S4 - 1:-1], T.m4[:], T.win[:, w + H0 + 511:w + H0 - 1:-1], 0.0, A.mult, A.max))
+        need("cv", k_mc, k_p)
+        for m in range(1, 7):
+            mk = T.mc[:, 128 * (m - 1) + 1:128 * m]
+            ep = w + EX + 256 * m
+            es = ep + 128
+            done("cv", v.tensor_tensor_scan(T.win[:, ep + 1:ep + 128], T.win[:, w + P4 + 3:w + P4 + 508:4], mk, 0.0, A.max, A.mult))
+            tok = done("cv", v.tensor_tensor_scan(T.win[:, es + 126:es - 1:-1], T.win[:, w + P4 + 511:w + P4 + 3:-4], mk, 0.0, A.max, A.mult))
+        return tok
+
+    WIN = [(H0, P4), (H0, P4 + 512), (H0, S4), (0, S4)]
+
+    def part(i, e, c, n):
+        lo, hi = WIN[e]
+        o = e * NS + c // 16
+        return T.win[:, i * WS + lo:i * WS + hi].indirect(T.ou[:, o:o + n // 16])
+
+    def gather(i, h, c, n, es, tab):
+        need("cs_", k_ou, tab)
+        w = len(es)
+        for e in es:
+            tok = done("cs_", s.activation(T["g%d%d" % (i, h)][:, e:w * n:w], part(i, e, c, n), F.Copy))
+        return tok
+
+    def merge(i, h, c, n, w, tok):
+        need("cv", k_m3, k_m2, tok)
+        src, dst = T["g%d%d" % (i, h)], T["s%d%d" % (i, h)]
+        msk = T.m3 if w == 3 else T.m2
+        k = done("cv", v.tensor_tensor_scan(dst[:, 0:w * n], msk[:, 0:w * n], src[:, 0:w * n], 0.0, A.mult, A.max))
+        cur = dst[:, w - 1:w * n:w]
+        if w == 2:
+            need("cv", k)
+            nxt = src[:, 0:n]
+            k = done("cv", v.tensor_tensor(nxt, part(i, 2, c, n), cur, A.max))
+            cur = nxt
+        need("cv", k)
+        return done("cv", v.tensor_tensor(T.tile[:, 4 * c + i:4 * (c + n):4], part(i, 3, c, n), cur, A.max))
+
+    t0 = tables(0)
+    g0 = gather(0, 0, 0, SL, (0, 1, 2), t0)
+    t1 = tables(1)
+    g1 = gather(1, 0, 0, SL, (0, 1, 2), t1)
+    t2 = tables(2)
+    merge(0, 0, 0, SL, 3, g0)
+    t3 = tables(3)
+    g20 = gather(2, 0, 0, HALF, (0, 1, 2), t2)
+    g30 = gather(3, 0, 0, HALF, (0, 1, 2), t3)
+    g21 = gather(2, 1, HALF, HALF, (0, 1), t2)
+    g31 = gather(3, 1, HALF, HALF, (0, 1, 2), t3)
+    merge(1, 0, 0, SL, 3, g1)
+    merge(2, 0, 0, HALF, 3, g20)
+    k = merge(3, 0, 0, HALF, 3, g30)
+    k_c0 = quant(T.cq[:, 0:HALF], T.cs[:, 0:HALF], T.tile[:, 0:4 * HALF], k)
+    merge(2, 1, HALF, HALF, 2, g21)
+    k = merge(3, 1, HALF, HALF, 3, g31)
+    k_c1 = quant(T.cq[:, HALF:SL], T.cs[:, HALF:SL], T.tile[:, 4 * HALF:4 * SL], k)
+
+    def place(q, r):
+        return (q - r - 1) % N
+
+    sent = 0
+    for tok, half in zip((k_c0, k_c1), sending(rank, T, topo)):
+        need("cg", tok)
+        for what in (0, 1):
+            trs = []
+            for j, r, es in half[what]:
+                dst = T.cores[r]
+                rid, pnc = topo.addr(dst)[0:2]
+                msk = 0
+                for e in es:
+                    msk |= 1 << e
+                b = 64 * place(rank, r)
+                if what == 0:
+                    src, out = T.cq[:, 64 * j:64 * j + 64].bitcast(dt.uint8), T.rq[:, b:b + 64].bitcast(dt.uint8)
+                else:
+                    src, out = T.cs[:, 64 * j:64 * j + 64], T.rs[:, b:b + 64]
+                trs.append(RemoteDMATransfer(dst_ids=[DstId(rid=rid, pnc=pnc)], dma_engine_mask=msk, remote_sem=T.sem.arr, src=src, dst=out))
+                sent += len(es)
+            g.remote_dma_fused(trs, local_sem=T.sem.sent)
+    arrive = 0
+    for q in range(N):
+        if q != rank:
+            for half in sending(q, T, topo):
+                for what in half:
+                    arrive += sum(len(es) for j, r, es in what if r == rank)
+
+    k_u = quant(T.uq[:], T.us[:], T.ub[:], ("uv", 32))
+    k_v = quant(T.vq[:], T.vs[:], T.vb[:], ("uv", 32))
+    back = 64 * (rank + 1)
+    need("cv", ("pfg", 256))
+    k = done("cv", v.tensor_scalar(T.pa[:], T.pl[:], -back, None, A.add))
+    k2 = done("cv", v.tensor_scalar(T.pz[:], T.pl[:, 16:32], 0, SL, A.is_lt, A.mult))
+    need("cv", k)
+    k = done("cv", v.tensor_scalar(T.pb[:], T.pa[:], 0, SL, A.is_lt, A.mult))
+    need("cv", k)
+    k = done("cv", v.tensor_tensor(T.pc[:], T.pa[:], T.pb[:], A.add))
+    need("cv", k)
+    k = done("cv", v.tensor_tensor(T.pc[:, 16:32], T.pc[:, 16:32], T.pz[:], A.max))
+    need("cv", k)
+    k_pu = done("cv", v.tensor_copy(T.pu[:], T.pc[:]))
+
+    own = slice(256, 384)
+    ku = mm(T.pp[:, 512:640], T.uq[:], T.us[:], T.cq[:, own], T.cs[:, own], k_c1, k_u)
+    kv = mm(T.pp[:, 0:128], T.vq[:], T.vs[:], T.cq[:, own], T.cs[:, own], k_v)
+    need("cs_", ku)
+    done("cs_", s.activation(T.zu[:, 320:384], T.pp[:, 576:640], F.Copy))
+    need("cs_", kv)
+    k_own = done("cs_", s.activation(T.zv[:, 320:384], T.pp[:, 64:128], F.Copy))
+
+    ku = mm(T.pp[:, 1536:1856], T.uq[:], T.us[:], T.rq[:], T.rs[:], ("arr", arrive))
+    kv = mm(T.pp[:, 1024:1344], T.vq[:], T.vs[:], T.rq[:], T.rs[:])
+    need("cs_", ku)
+    k_zc = done("cs_", s.activation(T.zu[:, 0:320], T.pp[:, 1536:1856], F.Copy))
+    need("cv", kv)
+    k_zv = done("cv", v.tensor_copy(T.zv[:, 0:320], T.pp[:, 1024:1344]))
+    need("cs_", k_pu, k_zu, k_zc)
+    k_g = [done("cs_", s.activation(T.gu[:, 128 * h:128 * h + 128], T.zu[:].indirect(T.pu[:, 16 + 8 * h:24 + 8 * h]), F.Copy)) for h in (0, 1)]
+    need("cv", k_own, k_zv)
+    for h in (0, 1):
+        need("cv", k_g[h])
+        k = done("cv", v.tensor_tensor(T.yb[:, 128 * h:128 * h + 128], T.zv[:].indirect(T.pu[:, 8 * h:8 * h + 8]), T.gu[:, 128 * h:128 * h + 128], A.add))
+        need("sy", k)
+        g.sync.dma_start(T.y[:, 128 * h:128 * h + 128], T.yb[:, 128 * h:128 * h + 128]).then_inc(T.sem["y%d" % h], 16)
+    g.wait_ge(T.sem.sent, sent)
+    need("sy", ("cs_", count["cs_"]), ("ct", count["ct"]), ("cg", count["cg"]), ("y0", 16), ("y1", 16))

@@ -5,11 +5,14 @@ N, T_COLS, CAPP, P = 6, 512, 64, 256
 SL = N * CAPP
 NS = SL // 16
 HALF = SL // 2
+XC = 256
 H0 = 128
 EX = 640
 S4 = EX + 7 * 256
 P4 = S4 + 512
 WS = 3584
+
+WORK = {(0, 2): 3, (1, 2): 2, (2, 0): 3, (3, 0): 2, (2, 1): 3, (3, 1): 3}
 
 SCRATCH = {
     "xb": ("sbuf", [128, 2048], "bfloat16"), "ab": ("sbuf", [128, 2048], "bfloat16"),
@@ -23,7 +26,7 @@ SCRATCH = {
     "win": ("sbuf", [128, 4 * WS], "bfloat16"),
     "tile": ("sbuf", [128, 4 * SL], "bfloat16"),
     "ones": ("sbuf", [128, 1152], "bfloat16"), "m3": ("sbuf", [128, 1152], "bfloat16"),
-    "m2": ("sbuf", [128, 384], "bfloat16"), "m4": ("sbuf", [128, 512], "bfloat16"),
+    "m2": ("sbuf", [128, 768], "bfloat16"), "m4": ("sbuf", [128, 512], "bfloat16"),
     "mc": ("sbuf", [128, 6 * 128], "bfloat16"), "m7": ("sbuf", [128, 7 * NS], "bfloat16"),
     "lr": ("sbuf", [128, 2 * NS], "int32"), "ln_": ("sbuf", [128, NS], "int32"), "lm": ("sbuf", [128, NS], "int32"),
     "sh": ("sbuf", [128, 14 * NS], "int32"), "fl": ("sbuf", [128, 7 * NS], "bfloat16"),
@@ -31,45 +34,41 @@ SCRATCH = {
     "yy": ("sbuf", [128, 2 * NS], "float32"), "pm": ("sbuf", [128, NS], "float32"),
     "xm": ("sbuf", [128, 2 * NS], "float32"), "of": ("sbuf", [128, 4 * NS], "float32"),
     "ou": ("sbuf", [128, 4 * NS], "uint16"),
-    "pl": ("sbuf", [128, 32], "int32"), "pa": ("sbuf", [128, 32], "int32"), "pb": ("sbuf", [128, 32], "int32"),
+    "pl": ("sbuf", [128, 32], "int32"), "pa": ("sbuf", [128, 32], "int32"), "pb": ("sbuf", [128, 64], "int32"),
     "pc": ("sbuf", [128, 32], "int32"), "pz": ("sbuf", [128, 16], "int32"), "pu": ("sbuf", [128, 32], "uint16"),
     "zu": ("sbuf", [128, 400], "float32"), "zv": ("sbuf", [128, 384], "float32"),
     "gu": ("sbuf", [128, P], "float32"), "yb": ("sbuf", [128, P], "float32"),
     "zp": ("psum", [128, 2048], "float32"), "pp": ("psum", [128, 2048], "float32"),
 }
-for _k in ("00", "10", "20", "21", "30", "31"):
-    _n = 3 * (SL if _k in ("00", "10") else HALF)
-    SCRATCH["g" + _k] = ("sbuf", [128, _n], "bfloat16")
-    SCRATCH["s" + _k] = ("sbuf", [128, _n], "bfloat16")
-SEMAPHORES = ["cv", "cs_", "ct", "cg", "lists", "x0", "x1", "a0", "a1", "a2", "uv", "pfg", "y0", "y1", "arr", "sent"]
+for (_i, _h), _w in WORK.items():
+    _n = 3 * (SL if _h == 2 else HALF)
+    SCRATCH["g%d%d" % (_i, _h)] = ("sbuf", [128, _n], "bfloat16")
+    SCRATCH["s%d%d" % (_i, _h)] = ("sbuf", [128, _n], "bfloat16")
+SEMAPHORES = ["cv", "cs_", "ct", "cg", "lists", "x0", "x1", "a0", "a1", "a2", "uv", "pfg", "y0", "y1", "arr0", "arr1", "sent"]
 
 
-def slot_order(q, T, topo):
-    me = T.cores[q]
-    rest = [(q + d) % N for d in range(1, N)]
-    far = sorted(r for r in rest if topo.die(T.cores[r]) != topo.die(me))
-    near = [r for r in rest if topo.die(T.cores[r]) == topo.die(me)]
-    return far + near + [q]
+def halves(q):
+    a, b = list(range(N // 2)), list(range(N // 2, N))
+    return (b, a) if q in a else (a, b)
 
 
-def runs(order):
-    out = []
-    for k, r in enumerate(order):
-        if out and out[-1][1] + out[-1][2] == r:
-            out[-1][2] += 1
-        else:
-            out.append([k, r, 1])
-    return out
+def places(r):
+    far, near = halves(r)
+    k = near.index(r)
+    return far + near[k + 1:] + near[:k] + [r]
 
 
 def sending(q, T, topo):
-    order = slot_order(q, T, topo)
-    eng = topo.engines(T.cores[q], T.cores[order[0]])
-    ev, od = eng[0::2], eng[1::2]
-    k = len(ev) // 2
-    first = [ev[:k], ev[k:], od], [od[:k], od[k:], ev]
-    last = [ev, od], [od, ev]
-    return [[(j, order[j], e) for j, e in enumerate(es)] for es in first], [[(3 + j, order[3 + j], e) for j, e in enumerate(es)] for es in last]
+    out = []
+    for ranks in halves(q):
+        ds = [r for r in ranks if r != q]
+        eng = topo.engines(T.cores[q], T.cores[ds[0]])
+        ev, od = eng[0::2], eng[1::2]
+        k = len(ev) // 2
+        ds.sort(key=lambda r: topo.die(T.cores[r]) == topo.die(T.cores[q]))
+        es = ([ev[:k], ev[k:], od], [od[:k], od[k:], ev]) if len(ds) == 3 else ([ev, od], [od, ev])
+        out.append([[(r, e) for r, e in zip(ds, x)] for x in es])
+    return out
 
 
 def rank_program(g, core, T, topo):
@@ -93,16 +92,11 @@ def rank_program(g, core, T, topo):
         count[q] += 1
         return (q, count[q])
 
-    order = slot_order(rank, T, topo)
-    rn = runs(order)
-
-    for k, r, n in rn:
-        s.dma_start(T.ln_[:, 4 * k:4 * (k + n)], T.ln[:, 4 * r:4 * (r + n)]).then_inc(T.sem.lists, 16)
-        s.dma_start(T.lr[:, 4 * k:4 * (k + n)], T.lo[:, 4 * r:4 * (r + n)]).then_inc(T.sem.lists, 16)
-    L_LISTS = ("lists", 32 * len(rn))
-    g.sync.dma_start(T.xb[:, 0:1024], T.x[:, 0:1024]).then_inc(T.sem.x0, 16)
-    g.sync.dma_start(T.ab[:, 0:512], T.a[:, 0:512]).then_inc(T.sem.a0, 16)
-    g.sync.dma_start(T.xb[:, 1024:2048], T.x[:, 1024:2048]).then_inc(T.sem.x1, 16)
+    s.dma_start(T.ln_[:], T.ln[:]).then_inc(T.sem.lists, 16)
+    g.sync.dma_start(T.lr[:, 0:NS], T.lo[:]).then_inc(T.sem.lists, 16)
+    g.sync.dma_start(T.xb[:, 0:4 * XC], T.x[:, 0:4 * XC]).then_inc(T.sem.x0, 16)
+    s.dma_start(T.ab[:, 0:512], T.a[:, 0:512]).then_inc(T.sem.a0, 16)
+    g.sync.dma_start(T.xb[:, 4 * XC:2048], T.x[:, 4 * XC:2048]).then_inc(T.sem.x1, 16)
     g.sync.dma_start(T.ab[:, 512:1024], T.a[:, 512:1024]).then_inc(T.sem.a1, 16)
     g.sync.dma_start(T.ab[:, 1024:2048], T.a[:, 1024:2048]).then_inc(T.sem.a2, 16)
     g.sync.dma_start(T.ub[:], T.u[:]).then_inc(T.sem.uv, 16)
@@ -134,19 +128,19 @@ def rank_program(g, core, T, topo):
     for m in range(1, 7):
         k_mc = mask(T.mc[:, 128 * (m - 1):128 * m], 128, 1 << m)
     k_m3 = mask(T.m3[:], 1152, 3)
-    k_m2 = mask(T.m2[:], 384, 2)
+    k_m2 = mask(T.m2[:], 768, 2)
 
-    need("cv", L_LISTS)
+    need("cv", ("lists", 32))
     k = done("cv", v.tensor_scalar(T.lm[:], T.ln_[:], -1, None, A.add))
     done("cv", v.tensor_scalar(T.ee[:, 0:NS], T.ln_[:], 2, -1, A.min, A.add))
-    k_ee = done("cv", v.tensor_scalar(T.ee[:, NS:2 * NS], T.ln_[:], 2, -(1 + H0), A.min, A.add))
+    done("cv", v.tensor_scalar(T.ee[:, NS:2 * NS], T.ln_[:], 2, -(1 + H0), A.min, A.add))
     need("cv", k)
     k_lr = done("cv", v.tensor_tensor(T.lr[:, NS:2 * NS], T.lr[:, 0:NS], T.lm[:], A.add))
     need("cv", k_lr)
     for j in range(7):
         k_sh = done("cv", v.tensor_scalar(T.sh[:, j::7], T.lr[:], 2 + j, None, A.arith_shift_right))
     done("cv", v.tensor_tensor(T.yy[:, 0:NS], T.lr[:, 0:NS], T.ee[:, 0:NS], A.add))
-    k_yy = done("cv", v.tensor_tensor(T.yy[:, NS:2 * NS], T.lr[:, NS:2 * NS], T.ee[:, NS:2 * NS], A.subtract))
+    done("cv", v.tensor_tensor(T.yy[:, NS:2 * NS], T.lr[:, NS:2 * NS], T.ee[:, NS:2 * NS], A.subtract))
     need("cv", k_sh)
     k_fl = done("cv", v.tensor_tensor(T.fl[:], T.sh[:, 0:7 * NS], T.sh[:, 7 * NS:14 * NS], A.not_equal))
 
@@ -154,15 +148,12 @@ def rank_program(g, core, T, topo):
         need("cv", *deps)
         return done("cv", v.quantize_mx(out, sc, src))
 
-    k_x0 = quant(T.xq[:, 0:256], T.xs[:, 0:256], T.xb[:, 0:1024], ("x0", 16))
-    k_a = [quant(T.aq[:, 0:128], T.sa[:, 0:128], T.ab[:, 0:512], ("a0", 16))]
-    k_x1 = quant(T.xq[:, 256:512], T.xs[:, 256:512], T.xb[:, 1024:2048], ("x1", 16))
-
+    k_x0 = quant(T.xq[:, 0:XC], T.xs[:, 0:XC], T.xb[:, 0:4 * XC], ("x0", 16))
     need("cv", k_fl)
     k_cn = done("cv", v.tensor_tensor_scan(T.cn[:], T.m7[:], T.fl[:], 0.0, A.mult, A.add))
+    k_a = [quant(T.aq[:, 0:128], T.sa[:, 0:128], T.ab[:, 0:512], ("a0", 16))]
     done("cv", v.tensor_scalar(T.of[:, 0:NS], T.fl[:, 0::7], S4 - H0, None, A.mult))
     k_of = done("cv", v.tensor_scalar(T.of[:, NS:2 * NS], T.fl[:, 0::7], P4 - H0, None, A.mult))
-    k_a.append(quant(T.aq[:, 128:256], T.sa[:, 128:256], T.ab[:, 512:1024], ("a1", 16)))
     need("cv", k_cn)
     k_pm = done("cv", v.tensor_scalar(T.pm[:], T.cn[:, 6::7], 256, None, A.mult))
     need("cv", k_of)
@@ -170,12 +161,9 @@ def rank_program(g, core, T, topo):
     need("cv", k_pm)
     done("cv", v.tensor_tensor(T.xm[:, 0:NS], T.sh[:, 0:7 * NS:7], T.pm[:], A.add))
     k_xm = done("cv", v.tensor_tensor(T.xm[:, NS:2 * NS], T.sh[:, 7 * NS:14 * NS:7], T.pm[:], A.add))
-    k_a.append(quant(T.aq[:, 256:512], T.sa[:, 256:512], T.ab[:, 1024:2048], ("a2", 16)))
-    k_a.append(k_a[2])
+    k_x1 = quant(T.xq[:, XC:512], T.xs[:, XC:512], T.xb[:, 4 * XC:2048], ("x1", 16))
     need("cv", k_xm)
-    k = done("cv", v.tensor_tensor(T.of[:, 2 * NS:4 * NS], T.xm[:], T.yy[:], A.max))
-    need("cv", k)
-    k_ou = done("cv", v.tensor_copy(T.ou[:], T.of[:]))
+    k_max = done("cv", v.tensor_tensor(T.of[:, 2 * NS:4 * NS], T.xm[:], T.yy[:], A.max))
 
     def mm(out, w, ws, x, xs, *deps):
         need("ct", *deps)
@@ -186,22 +174,27 @@ def rank_program(g, core, T, topo):
         b = i * WS + H0 + c
         return done("cs_", s.activation(T.win[:, b:b + n], src, F.Relu, scale=0.05))
 
-    k0 = mm(T.zp[:, 0:256], T.aq[:, 0:128], T.sa[:, 0:128], T.xq[:, 0:256], T.xs[:, 0:256], k_a[0])
-    k1 = mm(T.pp[:, 1536:1792], T.aq[:, 0:128], T.sa[:, 0:128], T.xq[:, 256:512], T.xs[:, 256:512], k_x1)
-    k_h = [[relu(0, 0, 256, T.zp[:, 0:256], k_win, k0), relu(0, 256, 256, T.pp[:, 1536:1792], k1)]]
-    for i in (1, 2, 3):
-        kk = mm(T.zp[:, 512 * i:512 * i + 512], T.aq[:, 128 * i:128 * i + 128], T.sa[:, 128 * i:128 * i + 128], T.xq[:], T.xs[:], k_a[i])
-        k_h.append([relu(i, 0, 512, T.zp[:, 512 * i:512 * i + 512], kk)])
+    k0 = mm(T.zp[:, 0:XC], T.aq[:, 0:128], T.sa[:, 0:128], T.xq[:, 0:XC], T.xs[:, 0:XC], k_x0, k_a[0])
+    k1 = mm(T.pp[:, 1536:2048 - XC], T.aq[:, 0:128], T.sa[:, 0:128], T.xq[:, XC:512], T.xs[:, XC:512], k_x1)
+    k_h = [[relu(0, 0, XC, T.zp[:, 0:XC], k_win, k0), relu(0, XC, 512 - XC, T.pp[:, 1536:2048 - XC], k1)]]
 
-    def tables(i):
+    def product(i):
+        return mm(T.zp[:, 512 * i:512 * i + 512], T.aq[:, 128 * i:128 * i + 128], T.sa[:, 128 * i:128 * i + 128], T.xq[:], T.xs[:], k_a[i])
+
+    def empty(i, k):
+        k_h.append([relu(i, 0, 512, T.zp[:, 512 * i:512 * i + 512], k)])
+
+    def prefix(i, j, a, b):
         w = i * WS
-        need("cv", k_m4)
-        step = T_COLS // len(k_h[i])
-        for c, kh in enumerate(k_h[i]):
-            need("cv", kh)
-            a, b = c * step, (c + 1) * step
-            k_p = done("cv", v.tensor_tensor_scan(T.win[:, w + P4 + a:w + P4 + b], T.m4[:, a:b], T.win[:, w + H0 + a:w + H0 + b], 0.0, A.mult, A.max))
-        done("cv", v.tensor_tensor_scan(T.win[:, w + S4 + 511:w + S4 - 1:-1], T.m4[:], T.win[:, w + H0 + 511:w + H0 - 1:-1], 0.0, A.mult, A.max))
+        need("cv", k_m4, k_h[i][j])
+        return done("cv", v.tensor_tensor_scan(T.win[:, w + P4 + a:w + P4 + b], T.m4[:, a:b], T.win[:, w + H0 + a:w + H0 + b], 0.0, A.mult, A.max))
+
+    def suffix(i):
+        w = i * WS
+        return done("cv", v.tensor_tensor_scan(T.win[:, w + S4 + 511:w + S4 - 1:-1], T.m4[:], T.win[:, w + H0 + 511:w + H0 - 1:-1], 0.0, A.mult, A.max))
+
+    def coarse(i, k_p):
+        w = i * WS
         need("cv", k_mc, k_p)
         for m in range(1, 7):
             mk = T.mc[:, 128 * (m - 1) + 1:128 * m]
@@ -211,114 +204,149 @@ def rank_program(g, core, T, topo):
             tok = done("cv", v.tensor_tensor_scan(T.win[:, es + 126:es - 1:-1], T.win[:, w + P4 + 511:w + P4 + 3:-4], mk, 0.0, A.max, A.mult))
         return tok
 
+    def tables(i):
+        k_p = prefix(i, 0, 0, 512)
+        suffix(i)
+        return coarse(i, k_p)
+
     WIN = [(H0, P4), (H0, P4 + 512), (H0, S4), (0, S4)]
+    base = [CAPP * r[0] for r in halves(rank)] + [0]
 
     def part(i, e, c, n):
         lo, hi = WIN[e]
         o = e * NS + c // 16
         return T.win[:, i * WS + lo:i * WS + hi].indirect(T.ou[:, o:o + n // 16])
 
-    def gather(i, h, c, n, es, tab):
+    def gather(i, h, tab, lists=(0, 1, 2)):
         need("cs_", k_ou, tab)
-        w = len(es)
-        for e in es:
-            tok = done("cs_", s.activation(T["g%d%d" % (i, h)][:, e:w * n:w], part(i, e, c, n), F.Copy))
+        w, c, n = WORK[i, h], base[h], SL if h == 2 else HALF
+        for e in lists:
+            if e < w:
+                tok = done("cs_", s.activation(T["g%d%d" % (i, h)][:, e:w * n:w], part(i, e, c, n), F.Copy))
         return tok
 
-    def merge(i, h, c, n, w, tok):
-        need("cv", k_m3, k_m2, tok)
-        src, dst = T["g%d%d" % (i, h)], T["s%d%d" % (i, h)]
-        msk = T.m3 if w == 3 else T.m2
+    def best(i, h, tok):
+        w, c, n = WORK[i, h], base[h], SL if h == 2 else HALF
+        need("cv", k_m3 if w == 3 else k_m2, tok)
+        msk, src, dst = T.m3 if w == 3 else T.m2, T["g%d%d" % (i, h)], T["s%d%d" % (i, h)]
         k = done("cv", v.tensor_tensor_scan(dst[:, 0:w * n], msk[:, 0:w * n], src[:, 0:w * n], 0.0, A.mult, A.max))
-        cur = dst[:, w - 1:w * n:w]
         if w == 2:
             need("cv", k)
-            nxt = src[:, 0:n]
-            k = done("cv", v.tensor_tensor(nxt, part(i, 2, c, n), cur, A.max))
-            cur = nxt
+            k = done("cv", v.tensor_tensor(src[:, 0:n], part(i, 2, c, n), dst[:, 1:2 * n:2], A.max))
+        return k
+
+    def last(i, h, k):
+        w, c, n = WORK[i, h], base[h], SL if h == 2 else HALF
         need("cv", k)
+        cur = T["s%d%d" % (i, h)][:, 2:3 * n:3] if w == 3 else T["g%d%d" % (i, h)][:, 0:n]
         return done("cv", v.tensor_tensor(T.tile[:, 4 * c + i:4 * (c + n):4], part(i, 3, c, n), cur, A.max))
 
-    t0 = tables(0)
-    g0 = gather(0, 0, 0, SL, (0, 1, 2), t0)
-    t1 = tables(1)
-    g1 = gather(1, 0, 0, SL, (0, 1, 2), t1)
-    t2 = tables(2)
-    merge(0, 0, 0, SL, 3, g0)
-    t3 = tables(3)
-    g20 = gather(2, 0, 0, HALF, (0, 1, 2), t2)
-    g30 = gather(3, 0, 0, HALF, (0, 1, 2), t3)
-    g21 = gather(2, 1, HALF, HALF, (0, 1), t2)
-    g31 = gather(3, 1, HALF, HALF, (0, 1, 2), t3)
-    merge(1, 0, 0, SL, 3, g1)
-    merge(2, 0, 0, HALF, 3, g20)
-    k = merge(3, 0, 0, HALF, 3, g30)
-    k_c0 = quant(T.cq[:, 0:HALF], T.cs[:, 0:HALF], T.tile[:, 0:4 * HALF], k)
-    merge(2, 1, HALF, HALF, 2, g21)
-    k = merge(3, 1, HALF, HALF, 3, g31)
-    k_c1 = quant(T.cq[:, HALF:SL], T.cs[:, HALF:SL], T.tile[:, 4 * HALF:4 * SL], k)
+    def pack(h, k):
+        c = base[h]
+        return quant(T.cq[:, c:c + HALF], T.cs[:, c:c + HALF], T.tile[:, 4 * c:4 * (c + HALF)], k)
 
-    def place(q, r):
-        return (q - r - 1) % N
+    prefix(0, 0, 0, XC)
+    need("cv", k_max)
+    k_ou = done("cv", v.tensor_copy(T.ou[:], T.of[:]))
+    kp = prefix(0, 1, XC, 512)
+    suffix(0)
+    k_a.append(quant(T.aq[:, 128:256], T.sa[:, 128:256], T.ab[:, 512:1024], ("a1", 16)))
+    empty(1, product(1))
+    t0 = coarse(0, kp)
+    k_a.append(quant(T.aq[:, 256:512], T.sa[:, 256:512], T.ab[:, 1024:2048], ("a2", 16)))
+    k_a.append(k_a[2])
+    z2, z3 = product(2), product(3)
+    gather(0, 2, t0, (0,))
+    empty(2, z2)
+    t1 = tables(1)
+    g0 = gather(0, 2, t0, (1, 2))
+    empty(3, z3)
+    t2 = tables(2)
+    g1 = gather(1, 2, t1)
+    b0 = best(0, 2, g0)
+    kp = prefix(3, 0, 0, 512)
+    last(0, 2, b0)
+    suffix(3)
+    t3 = coarse(3, kp)
+    g20, g30 = gather(2, 0, t2), gather(3, 0, t3)
+    g21, g31 = gather(2, 1, t2), gather(3, 1, t3)
+    last(1, 2, best(1, 2, g1))
+    last(2, 0, best(2, 0, g20))
+    k_c0 = pack(0, last(3, 0, best(3, 0, g30)))
+    b21 = best(2, 1, g21)
+    b31 = best(3, 1, g31)
+    last(2, 1, b21)
+    k_c1 = pack(1, last(3, 1, b31))
 
     sent = 0
-    for tok, half in zip((k_c0, k_c1), sending(rank, T, topo)):
+    for h, (tok, half) in enumerate(zip((k_c0, k_c1), sending(rank, T, topo))):
         need("cg", tok)
         for what in (0, 1):
             trs = []
-            for j, r, es in half[what]:
-                dst = T.cores[r]
-                rid, pnc = topo.addr(dst)[0:2]
+            for r, es in half[what]:
+                rid, pnc = topo.addr(T.cores[r])[0:2]
                 msk = 0
                 for e in es:
                     msk |= 1 << e
-                b = 64 * place(rank, r)
+                a, b = CAPP * r, CAPP * places(r).index(rank)
                 if what == 0:
-                    src, out = T.cq[:, 64 * j:64 * j + 64].bitcast(dt.uint8), T.rq[:, b:b + 64].bitcast(dt.uint8)
+                    src, out = T.cq[:, a:a + CAPP].bitcast(dt.uint8), T.rq[:, b:b + CAPP].bitcast(dt.uint8)
                 else:
-                    src, out = T.cs[:, 64 * j:64 * j + 64], T.rs[:, b:b + 64]
-                trs.append(RemoteDMATransfer(dst_ids=[DstId(rid=rid, pnc=pnc)], dma_engine_mask=msk, remote_sem=T.sem.arr, src=src, dst=out))
+                    src, out = T.cs[:, a:a + CAPP], T.rs[:, b:b + CAPP]
+                trs.append(RemoteDMATransfer(dst_ids=[DstId(rid=rid, pnc=pnc)], dma_engine_mask=msk, remote_sem=T.sem["arr%d" % h], src=src, dst=out))
                 sent += len(es)
             g.remote_dma_fused(trs, local_sem=T.sem.sent)
-    arrive = 0
+    arrive = [0, 0]
     for q in range(N):
         if q != rank:
-            for half in sending(q, T, topo):
+            for h, half in enumerate(sending(q, T, topo)):
                 for what in half:
-                    arrive += sum(len(es) for j, r, es in what if r == rank)
+                    arrive[h] += sum(len(es) for r, es in what if r == rank)
 
     k_u = quant(T.uq[:], T.us[:], T.ub[:], ("uv", 32))
     k_v = quant(T.vq[:], T.vs[:], T.vb[:], ("uv", 32))
-    back = 64 * (rank + 1)
+    shift = [CAPP * (places(rank).index(q) - q) for q in range(N)]
+    steps = [(CAPP * q, shift[q - 1] - shift[q]) for q in range(1, N) if shift[q - 1] != shift[q]]
     need("cv", ("pfg", 256))
-    k = done("cv", v.tensor_scalar(T.pa[:], T.pl[:], -back, None, A.add))
-    k2 = done("cv", v.tensor_scalar(T.pz[:], T.pl[:, 16:32], 0, SL, A.is_lt, A.mult))
+    done("cv", v.tensor_scalar(T.pa[:], T.pl[:], shift[N - 1], None, A.add))
+    for j, (b, d) in enumerate(steps):
+        done("cv", v.tensor_scalar(T.pb[:, 32 * j:32 * j + 32], T.pl[:], b, d, A.is_lt, A.mult))
+    k = done("cv", v.tensor_scalar(T.pz[:], T.pl[:, 16:32], 0, SL, A.is_lt, A.mult))
+    cur = T.pa
+    for j in range(len(steps)):
+        need("cv", k)
+        nxt = T.pc if cur is T.pa else T.pa
+        k = done("cv", v.tensor_tensor(nxt[:], cur[:], T.pb[:, 32 * j:32 * j + 32], A.add))
+        cur = nxt
     need("cv", k)
-    k = done("cv", v.tensor_scalar(T.pb[:], T.pa[:], 0, SL, A.is_lt, A.mult))
+    k = done("cv", v.tensor_tensor(cur[:, 16:32], cur[:, 16:32], T.pz[:], A.max))
     need("cv", k)
-    k = done("cv", v.tensor_tensor(T.pc[:], T.pa[:], T.pb[:], A.add))
-    need("cv", k)
-    k = done("cv", v.tensor_tensor(T.pc[:, 16:32], T.pc[:, 16:32], T.pz[:], A.max))
-    need("cv", k)
-    k_pu = done("cv", v.tensor_copy(T.pu[:], T.pc[:]))
+    k_pu = done("cv", v.tensor_copy(T.pu[:], cur[:]))
 
-    own = slice(256, 384)
-    ku = mm(T.pp[:, 512:640], T.uq[:], T.us[:], T.cq[:, own], T.cs[:, own], k_c1, k_u)
-    kv = mm(T.pp[:, 0:128], T.vq[:], T.vs[:], T.cq[:, own], T.cs[:, own], k_v)
+    ob = min(CAPP * rank, base[1] + HALF - 128)
+    oc = CAPP * rank - ob
+    ku = mm(T.pp[:, 0:HALF], T.uq[:], T.us[:], T.rq[:, 0:HALF], T.rs[:, 0:HALF], k_u, ("arr0", arrive[0]))
+    kv = mm(T.pp[:, 512:512 + HALF], T.vq[:], T.vs[:], T.rq[:, 0:HALF], T.rs[:, 0:HALF], k_v)
+    kuo = mm(T.pp[:, 1024:1152], T.uq[:], T.us[:], T.cq[:, ob:ob + 128], T.cs[:, ob:ob + 128], k_c1)
+    kvo = mm(T.pp[:, 1536:1664], T.vq[:], T.vs[:], T.cq[:, ob:ob + 128], T.cs[:, ob:ob + 128])
     need("cs_", ku)
-    done("cs_", s.activation(T.zu[:, 320:384], T.pp[:, 576:640], F.Copy))
-    need("cs_", kv)
-    k_own = done("cs_", s.activation(T.zv[:, 320:384], T.pp[:, 64:128], F.Copy))
-
-    ku = mm(T.pp[:, 1536:1856], T.uq[:], T.us[:], T.rq[:], T.rs[:], ("arr", arrive))
-    kv = mm(T.pp[:, 1024:1344], T.vq[:], T.vs[:], T.rq[:], T.rs[:])
-    need("cs_", ku)
-    k_zc = done("cs_", s.activation(T.zu[:, 0:320], T.pp[:, 1536:1856], F.Copy))
+    done("cs_", s.activation(T.zu[:, 0:HALF], T.pp[:, 0:HALF], F.Copy))
+    need("cs_", kuo)
+    k_uo = done("cs_", s.activation(T.zu[:, 320:384], T.pp[:, 1024 + oc:1024 + oc + CAPP], F.Copy))
     need("cv", kv)
-    k_zv = done("cv", v.tensor_copy(T.zv[:, 0:320], T.pp[:, 1024:1344]))
-    need("cs_", k_pu, k_zu, k_zc)
+    done("cv", v.tensor_copy(T.zv[:, 0:HALF], T.pp[:, 512:512 + HALF]))
+    need("cv", kvo)
+    k_vo = done("cv", v.tensor_copy(T.zv[:, 320:384], T.pp[:, 1536 + oc:1536 + oc + CAPP]))
+
+    ku = mm(T.zp[:, 0:128], T.uq[:], T.us[:], T.rq[:, HALF:320], T.rs[:, HALF:320], ("arr1", arrive[1]))
+    kv = mm(T.zp[:, 512:640], T.vq[:], T.vs[:], T.rq[:, HALF:320], T.rs[:, HALF:320])
+    need("cs_", ku)
+    k_zu2 = done("cs_", s.activation(T.zu[:, HALF:320], T.zp[:, 0:128], F.Copy))
+    need("cv", kv)
+    k_zv = done("cv", v.tensor_copy(T.zv[:, HALF:320], T.zp[:, 512:640]))
+    need("cs_", k_pu, k_zu2)
     k_g = [done("cs_", s.activation(T.gu[:, 128 * h:128 * h + 128], T.zu[:].indirect(T.pu[:, 16 + 8 * h:24 + 8 * h]), F.Copy)) for h in (0, 1)]
-    need("cv", k_own, k_zv)
+    need("cv", k_zv)
     for h in (0, 1):
         need("cv", k_g[h])
         k = done("cv", v.tensor_tensor(T.yb[:, 128 * h:128 * h + 128], T.zv[:].indirect(T.pu[:, 8 * h:8 * h + 8]), T.gu[:, 128 * h:128 * h + 128], A.add))

@@ -4,15 +4,22 @@ from concourse.mybir import dt, AluOpType, ActivationFunctionType
 N, T_COLS, CAPP, P = 6, 512, 64, 256
 SL = N * CAPP
 NS = SL // 16
-HALF = SL // 2
-XC = 256
-H0 = 128
-EX = 640
-S4 = EX + 7 * 256
-P4 = S4 + 512
-WS = 3584
+CC = CAPP // 16
+B = 6
+ST = 528
+NB = ST // B
+LV = 6
+XC = 43 * B
+S6, P6 = 2 * ST, 4 * ST
+W = 4768
+CE, DE = -ST, -3 * ST
+EP, ES = W + DE, W + CE
+RG = ES + 2 * ST
 
-WORK = {(0, 2): 3, (1, 2): 2, (2, 0): 3, (3, 0): 2, (2, 1): 3, (3, 1): 3}
+FAR, NEAR = 3 * CAPP, 2 * CAPP
+CH = {"a": (0, FAR + NEAR), "f": (0, FAR), "n": (FAR, NEAR), "o": (FAR + NEAR, CAPP)}
+WORK = {(0, "a"): 3, (1, "f"): 3, (2, "f"): 3, (3, "f"): 3, (1, "n"): 3, (2, "n"): 3, (3, "n"): 3,
+        (0, "o"): 3, (1, "o"): 3, (2, "o"): 3, (3, "o"): 3}
 
 SCRATCH = {
     "xb": ("sbuf", [128, 2048], "bfloat16"), "ab": ("sbuf", [128, 2048], "bfloat16"),
@@ -21,51 +28,57 @@ SCRATCH = {
     "aq": ("sbuf", [128, 512], "float8_e4m3fn_x4"), "sa": ("sbuf", [128, 512], "uint8"),
     "uq": ("sbuf", [128, 128], "float8_e4m3fn_x4"), "us": ("sbuf", [128, 128], "uint8"),
     "vq": ("sbuf", [128, 128], "float8_e4m3fn_x4"), "vs": ("sbuf", [128, 128], "uint8"),
-    "cq": ("sbuf", [128, SL], "float8_e4m3fn_x4"), "cs": ("sbuf", [128, SL], "uint8"),
+    "cq": ("sbuf", [128, 320], "float8_e4m3fn_x4"), "cs": ("sbuf", [128, 320], "uint8"),
+    "oq": ("sbuf", [128, 128], "float8_e4m3fn_x4"), "ow": ("sbuf", [128, 128], "uint8"),
     "rq": ("sbuf", [128, 320], "float8_e4m3fn_x4"), "rs": ("sbuf", [128, 320], "uint8"),
-    "win": ("sbuf", [128, 4 * WS], "bfloat16"),
+    "win": ("sbuf", [128, 2 * RG], "bfloat16"),
     "tile": ("sbuf", [128, 4 * SL], "bfloat16"),
-    "ones": ("sbuf", [128, 1152], "bfloat16"), "m3": ("sbuf", [128, 1152], "bfloat16"),
-    "m2": ("sbuf", [128, 768], "bfloat16"), "m4": ("sbuf", [128, 512], "bfloat16"),
-    "mc": ("sbuf", [128, 6 * 128], "bfloat16"), "m7": ("sbuf", [128, 7 * NS], "bfloat16"),
-    "lr": ("sbuf", [128, 2 * NS], "int32"), "ln_": ("sbuf", [128, NS], "int32"), "lm": ("sbuf", [128, NS], "int32"),
-    "sh": ("sbuf", [128, 14 * NS], "int32"), "fl": ("sbuf", [128, 7 * NS], "bfloat16"),
-    "cn": ("sbuf", [128, 7 * NS], "bfloat16"), "ee": ("sbuf", [128, 2 * NS], "float32"),
-    "yy": ("sbuf", [128, 2 * NS], "float32"), "pm": ("sbuf", [128, NS], "float32"),
-    "xm": ("sbuf", [128, 2 * NS], "float32"), "of": ("sbuf", [128, 4 * NS], "float32"),
-    "ou": ("sbuf", [128, 4 * NS], "uint16"),
-    "pl": ("sbuf", [128, 32], "int32"), "pa": ("sbuf", [128, 32], "int32"), "pb": ("sbuf", [128, 64], "int32"),
-    "pc": ("sbuf", [128, 32], "int32"), "pz": ("sbuf", [128, 16], "int32"), "pu": ("sbuf", [128, 32], "uint16"),
+    "ones": ("sbuf", [128, 960], "bfloat16"), "m6": ("sbuf", [128, ST], "bfloat16"),
+    "m3": ("sbuf", [128, 960], "bfloat16"), "m2": ("sbuf", [128, 640], "bfloat16"),
+    "mc": ("sbuf", [128, 6 * 2 * NB], "bfloat16"), "aw": ("sbuf", [128, LV * NS], "bfloat16"),
+    "ll": ("sbuf", [128, 2 * NS], "int32"), "lm": ("sbuf", [128, NS], "float32"),
+    "ld": ("sbuf", [128, 4 * NS], "float32"), "l6": ("sbuf", [128, 2 * NS], "int32"), "sb": ("sbuf", [128, 2 * NS], "int32"),
+    "sh": ("sbuf", [128, 2 * LV * NS], "int32"), "fl": ("sbuf", [128, LV * NS], "bfloat16"),
+    "cn": ("sbuf", [128, LV * NS], "float32"), "ee": ("sbuf", [128, 2 * NS], "float32"),
+    "yy": ("sbuf", [128, 2 * NS], "float32"), "xm": ("sbuf", [128, 2 * NS], "float32"),
+    "dd": ("sbuf", [128, 2 * NS], "float32"), "fd": ("sbuf", [128, 2 * NS], "float32"),
+    "of": ("sbuf", [128, 4 * NS], "float32"), "oa": ("sbuf", [128, 2 * NS], "uint16"), "oc": ("sbuf", [128, 2 * NS], "uint16"),
+    "pl": ("sbuf", [128, 32], "int32"), "pz": ("sbuf", [128, 16], "int32"), "pu": ("sbuf", [128, 32], "uint16"),
     "zu": ("sbuf", [128, 400], "float32"), "zv": ("sbuf", [128, 384], "float32"),
     "gu": ("sbuf", [128, P], "float32"), "yb": ("sbuf", [128, P], "float32"),
     "zp": ("psum", [128, 2048], "float32"), "pp": ("psum", [128, 2048], "float32"),
 }
 for (_i, _h), _w in WORK.items():
-    _n = 3 * (SL if _h == 2 else HALF)
-    SCRATCH["g%d%d" % (_i, _h)] = ("sbuf", [128, _n], "bfloat16")
-    SCRATCH["s%d%d" % (_i, _h)] = ("sbuf", [128, _n], "bfloat16")
+    SCRATCH["g%d%s" % (_i, _h)] = ("sbuf", [128, _w * CH[_h][1]], "bfloat16")
+    SCRATCH["s%d%s" % (_i, _h)] = ("sbuf", [128, _w * CH[_h][1]], "bfloat16")
 SEMAPHORES = ["cv", "cs_", "ct", "cg", "lists", "x0", "x1", "a0", "a1", "a2", "uv", "pfg", "y0", "y1", "arr0", "arr1", "sent"]
 
 
-def halves(q):
-    a, b = list(range(N // 2)), list(range(N // 2, N))
-    return (b, a) if q in a else (a, b)
+def order(q):
+    return [(q + 1 + k) % N for k in range(N)]
 
 
 def places(r):
-    far, near = halves(r)
-    k = near.index(r)
-    return far + near[k + 1:] + near[:k] + [r]
+    return [(r + 3 + k) % N for k in range(3)] + [(r + 1 + k) % N for k in range(2)]
+
+
+def runs(ranks):
+    out = []
+    for k, q in enumerate(ranks):
+        if out and out[-1][1] + out[-1][2] == q:
+            out[-1][2] += 1
+        else:
+            out.append([k, q, 1])
+    return out
 
 
 def sending(q, T, topo):
     out = []
-    for ranks in halves(q):
-        ds = [r for r in ranks if r != q]
+    for ds in (order(q)[0:3], order(q)[3:5]):
         eng = topo.engines(T.cores[q], T.cores[ds[0]])
         ev, od = eng[0::2], eng[1::2]
         k = len(ev) // 2
-        ds.sort(key=lambda r: topo.die(T.cores[r]) == topo.die(T.cores[q]))
+        ds = sorted(ds, key=lambda r: topo.die(T.cores[r]) == topo.die(T.cores[q]))
         es = ([ev[:k], ev[k:], od], [od[:k], od[k:], ev]) if len(ds) == 3 else ([ev, od], [od, ev])
         out.append([[(r, e) for r, e in zip(ds, x)] for x in es])
     return out
@@ -92,8 +105,8 @@ def rank_program(g, core, T, topo):
         count[q] += 1
         return (q, count[q])
 
-    s.dma_start(T.ln_[:], T.ln[:]).then_inc(T.sem.lists, 16)
-    g.sync.dma_start(T.lr[:, 0:NS], T.lo[:]).then_inc(T.sem.lists, 16)
+    s.dma_start(T.ll[:, NS:2 * NS], T.ln[:]).then_inc(T.sem.lists, 16)
+    g.sync.dma_start(T.ll[:, 0:NS], T.lo[:]).then_inc(T.sem.lists, 16)
     g.sync.dma_start(T.xb[:, 0:4 * XC], T.x[:, 0:4 * XC]).then_inc(T.sem.x0, 16)
     s.dma_start(T.ab[:, 0:512], T.a[:, 0:512]).then_inc(T.sem.a0, 16)
     g.sync.dma_start(T.xb[:, 4 * XC:2048], T.x[:, 4 * XC:2048]).then_inc(T.sem.x1, 16)
@@ -106,129 +119,162 @@ def rank_program(g, core, T, topo):
         g.sync.dma_start(T.pl[16 * k:16 * k + 16, 16:32], T.pg[:]).then_inc(T.sem.pfg, 16)
 
     k_one = done("cv", v.memset(T.ones[:], 1.0))
-    k_m7 = done("cv", v.memset(T.m7[:], 1.0))
-    for i in range(4):
-        done("cv", v.memset(T.win[:, i * WS:i * WS + H0], 0.0))
-        done("cv", v.memset(T.win[:, i * WS + EX:i * WS + EX + 256], 0.0))
-    need("cv", k_m7)
-    done("cv", v.memset(T.m7[:, 0::7], 0.0))
-    k_m7 = done("cv", v.memset(T.m7[:, 1::7], 2.5))
-    k_z = ("cv", count["cv"] - 2)
-    need("cv", k_z)
-    done("cv", v.memset(T.win[:, 128::256], 0.0))
-    k_win = done("cv", v.memset(T.win[:, 127::256], 0.0))
+    k_mo = done("cv", v.memset(T.mc[:, 3 * 2 * NB:6 * 2 * NB], 1.0))
+    k_aw = done("cv", v.memset(T.aw[:], 1.0))
     k_zu = done("cv", v.memset(T.zu[:, 384:400], 0.0))
+    need("cv", k_aw)
+    done("cv", v.memset(T.aw[:, 0::LV], 0.0))
+    k_aw = done("cv", v.memset(T.aw[:, 1::LV], float(W)))
 
     need("cg", k_one)
 
     def mask(out, n, b):
         return done("cg", g.affine_select(out, T.ones[:, 0:n], [[0, n // b], [1, b]], A.is_gt, 0.0, 0, 0))
 
-    k_m4 = mask(T.m4[:], 512, 4)
-    for m in range(1, 7):
-        k_mc = mask(T.mc[:, 128 * (m - 1):128 * m], 128, 1 << m)
-    k_m3 = mask(T.m3[:], 1152, 3)
-    k_m2 = mask(T.m2[:], 768, 2)
+    k_m6 = mask(T.m6[:], ST, B)
+    for m in range(1, 4):
+        k_mc = mask(T.mc[:, 2 * NB * (m - 1):2 * NB * m], 2 * NB, 1 << m)
+    k_ms = {3: mask(T.m3[:], 960, 3)}
+    if 2 in WORK.values():
+        k_ms[2] = mask(T.m2[:], 640, 2)
 
+    def zero(out, n):
+        return done("cs_", s.activation(out, T.ones[:, 0:n], F.Copy, scale=0.0))
+
+    need("cs_", k_one)
+    for i in range(4):
+        b = (i // 2) * RG + (i % 2) * ST
+        k_hp = zero(T.win[:, b + T_COLS:b + ST], ST - T_COLS)
+    for p in range(2):
+        zero(T.win[:, p * RG + 6 * ST:p * RG + EP + LV], EP + LV - 6 * ST)
+        zero(T.win[:, p * RG + ES + 2 * ST - LV:p * RG + RG], LV)
+    need("cs_", k_mo)
+    for m in range(4, 7):
+        for p in range(2):
+            b = 2 * NB * (m - 1) + NB * p
+            k_mz = zero(T.mc[:, b:b + NB:1 << m], len(range(0, NB, 1 << m)))
+
+    c = CC * ((rank + 1) % N)
+    cuts = [(0, c, NS - c)] + ([(NS - c, 0, c)] if c else [])
     need("cv", ("lists", 32))
-    k = done("cv", v.tensor_scalar(T.lm[:], T.ln_[:], -1, None, A.add))
-    done("cv", v.tensor_scalar(T.ee[:, 0:NS], T.ln_[:], 2, -1, A.min, A.add))
-    done("cv", v.tensor_scalar(T.ee[:, NS:2 * NS], T.ln_[:], 2, -(1 + H0), A.min, A.add))
+    for o, b, n in cuts:
+        done("cv", v.tensor_copy(T.ld[:, NS + o:NS + o + n], T.ll[:, b:b + n]))
+    for o, b, n in cuts:
+        k_lm = done("cv", v.tensor_scalar(T.lm[:, o:o + n], T.ll[:, NS + b:NS + b + n], -1, None, A.add))
+    LR = T.ld[:, NS:3 * NS]
+    need("cv", k_lm)
+    k = done("cv", v.tensor_tensor(T.ld[:, 2 * NS:3 * NS], T.ld[:, NS:2 * NS], T.lm[:], A.add))
     need("cv", k)
-    k_lr = done("cv", v.tensor_tensor(T.lr[:, NS:2 * NS], T.lr[:, 0:NS], T.lm[:], A.add))
-    need("cv", k_lr)
-    for j in range(7):
-        k_sh = done("cv", v.tensor_scalar(T.sh[:, j::7], T.lr[:], 2 + j, None, A.arith_shift_right))
-    done("cv", v.tensor_tensor(T.yy[:, 0:NS], T.lr[:, 0:NS], T.ee[:, 0:NS], A.add))
-    done("cv", v.tensor_tensor(T.yy[:, NS:2 * NS], T.lr[:, NS:2 * NS], T.ee[:, NS:2 * NS], A.subtract))
-    need("cv", k_sh)
-    k_fl = done("cv", v.tensor_tensor(T.fl[:], T.sh[:, 0:7 * NS], T.sh[:, 7 * NS:14 * NS], A.not_equal))
+    k = done("cv", v.tensor_scalar(T.l6[:], LR, 171, None, A.mult))
+    need("cs_", k_lm)
+    done("cs_", s.activation(T.ee[:, 0:NS], T.lm[:], F.Sign))
+    k_ee = done("cs_", s.activation(T.ee[:, NS:2 * NS], T.lm[:], F.Sign, scale=-1.0))
+    need("cv", k)
+    k = done("cv", v.tensor_scalar(T.sb[:], T.l6[:], 10, None, A.arith_shift_right))
+    for j in range(3):
+        done("cv", v.tensor_scalar(T.sh[:, j::LV], T.l6[:], 11 + j, None, A.arith_shift_right))
+    need("cv", k)
+    done("cv", v.tensor_scalar(T.ld[:, 0:NS], T.sb[:, 0:NS], B, CE, A.mult, A.add))
+    k_ld = done("cv", v.tensor_scalar(T.ld[:, 3 * NS:4 * NS], T.sb[:, NS:2 * NS], B, DE, A.mult, A.add))
 
     def quant(out, sc, src, *deps):
         need("cv", *deps)
         return done("cv", v.quantize_mx(out, sc, src))
 
     k_x0 = quant(T.xq[:, 0:XC], T.xs[:, 0:XC], T.xb[:, 0:4 * XC], ("x0", 16))
-    need("cv", k_fl)
-    k_cn = done("cv", v.tensor_tensor_scan(T.cn[:], T.m7[:], T.fl[:], 0.0, A.mult, A.add))
+    need("cv", k_ld)
+    k = done("cv", v.tensor_tensor(T.dd[:], T.ld[:, 0:2 * NS], T.ld[:, 2 * NS:4 * NS], A.subtract))
     k_a = [quant(T.aq[:, 0:128], T.sa[:, 0:128], T.ab[:, 0:512], ("a0", 16))]
-    done("cv", v.tensor_scalar(T.of[:, 0:NS], T.fl[:, 0::7], S4 - H0, None, A.mult))
-    k_of = done("cv", v.tensor_scalar(T.of[:, NS:2 * NS], T.fl[:, 0::7], P4 - H0, None, A.mult))
-    need("cv", k_cn)
-    k_pm = done("cv", v.tensor_scalar(T.pm[:], T.cn[:, 6::7], 256, None, A.mult))
-    need("cv", k_of)
-    done("cv", v.tensor_tensor(T.of[:, 0:2 * NS], T.of[:, 0:2 * NS], T.lr[:], A.add))
-    need("cv", k_pm)
-    done("cv", v.tensor_tensor(T.xm[:, 0:NS], T.sh[:, 0:7 * NS:7], T.pm[:], A.add))
-    k_xm = done("cv", v.tensor_tensor(T.xm[:, NS:2 * NS], T.sh[:, 7 * NS:14 * NS:7], T.pm[:], A.add))
+    need("cv", k)
+    done("cv", v.tensor_scalar(T.fd[:, 0:NS], T.dd[:, 0:NS], CE - (B - 1), S6, A.is_le, A.mult))
+    k = done("cv", v.tensor_scalar(T.fd[:, NS:2 * NS], T.dd[:, NS:2 * NS], -DE, P6, A.is_le, A.mult))
+    for j in range(3, LV):
+        k_sh = done("cv", v.tensor_scalar(T.sh[:, j::LV], T.l6[:], 11 + j, None, A.arith_shift_right))
+    need("cv", k)
+    k = done("cv", v.tensor_tensor(T.of[:, 0:2 * NS], LR, T.fd[:], A.add))
     k_x1 = quant(T.xq[:, XC:512], T.xs[:, XC:512], T.xb[:, 4 * XC:2048], ("x1", 16))
-    need("cv", k_xm)
-    k_max = done("cv", v.tensor_tensor(T.of[:, 2 * NS:4 * NS], T.xm[:], T.yy[:], A.max))
+    need("cv", k)
+    k_oa = done("cv", v.tensor_copy(T.oa[:], T.of[:, 0:2 * NS]))
+
+    def levels():
+        need("cv", k_sh)
+        return done("cv", v.tensor_tensor(T.fl[:], T.sh[:, 0:LV * NS], T.sh[:, LV * NS:2 * LV * NS], A.not_equal))
+
+    def offsets(k):
+        need("cv", k, k_aw)
+        k = done("cv", v.tensor_tensor_scan(T.cn[:], T.aw[:], T.fl[:], 0.0, A.mult, A.add))
+        need("cv", k_ee)
+        done("cv", v.tensor_tensor(T.yy[:], LR, T.ee[:], A.add))
+        need("cv", k)
+        done("cv", v.tensor_tensor(T.xm[:, 0:NS], T.ld[:, 0:NS], T.cn[:, LV - 1::LV], A.add))
+        k = done("cv", v.tensor_tensor(T.xm[:, NS:2 * NS], T.ld[:, 3 * NS:4 * NS], T.cn[:, LV - 1::LV], A.add))
+        need("cv", k)
+        k = done("cv", v.tensor_tensor(T.of[:, 2 * NS:4 * NS], T.xm[:], T.yy[:], A.max))
+        need("cv", k)
+        return done("cv", v.tensor_copy(T.oc[:], T.of[:, 2 * NS:4 * NS]))
 
     def mm(out, w, ws, x, xs, *deps):
         need("ct", *deps)
         return done("ct", t.matmul_mx(out, w, ws, x, xs, True, True))
 
+    def at(i):
+        return (i // 2) * RG + (i % 2) * ST
+
     def relu(i, c, n, src, *deps):
         need("cs_", *deps)
-        b = i * WS + H0 + c
-        return done("cs_", s.activation(T.win[:, b:b + n], src, F.Relu, scale=0.05))
+        return done("cs_", s.activation(T.win[:, at(i) + c:at(i) + c + n], src, F.Relu, scale=0.05))
 
     k0 = mm(T.zp[:, 0:XC], T.aq[:, 0:128], T.sa[:, 0:128], T.xq[:, 0:XC], T.xs[:, 0:XC], k_x0, k_a[0])
     k1 = mm(T.pp[:, 1536:2048 - XC], T.aq[:, 0:128], T.sa[:, 0:128], T.xq[:, XC:512], T.xs[:, XC:512], k_x1)
-    k_h = [[relu(0, 0, XC, T.zp[:, 0:XC], k_win, k0), relu(0, XC, 512 - XC, T.pp[:, 1536:2048 - XC], k1)]]
+    k_h = {0: relu(0, 0, XC, T.zp[:, 0:XC], k0), 4: relu(0, XC, 512 - XC, T.pp[:, 1536:2048 - XC], k1)}
 
     def product(i):
         return mm(T.zp[:, 512 * i:512 * i + 512], T.aq[:, 128 * i:128 * i + 128], T.sa[:, 128 * i:128 * i + 128], T.xq[:], T.xs[:], k_a[i])
 
     def empty(i, k):
-        k_h.append([relu(i, 0, 512, T.zp[:, 512 * i:512 * i + 512], k)])
+        k_h[i] = relu(i, 0, 512, T.zp[:, 512 * i:512 * i + 512], k)
 
-    def prefix(i, j, a, b):
-        w = i * WS
-        need("cv", k_m4, k_h[i][j])
-        return done("cv", v.tensor_tensor_scan(T.win[:, w + P4 + a:w + P4 + b], T.m4[:, a:b], T.win[:, w + H0 + a:w + H0 + b], 0.0, A.mult, A.max))
+    def prefix(i, a, b, *deps):
+        w = at(i)
+        need("cv", k_m6, k_hp, *deps)
+        return done("cv", v.tensor_tensor_scan(T.win[:, w + P6 + a:w + P6 + b], T.m6[:, a:b], T.win[:, w + a:w + b], 0.0, A.mult, A.max))
 
-    def suffix(i):
-        w = i * WS
-        return done("cv", v.tensor_tensor_scan(T.win[:, w + S4 + 511:w + S4 - 1:-1], T.m4[:], T.win[:, w + H0 + 511:w + H0 - 1:-1], 0.0, A.mult, A.max))
+    def suffix(i, *deps):
+        w = at(i)
+        need("cv", k_m6, k_hp, *deps)
+        end = w - 1 if w else None
+        return done("cv", v.tensor_tensor_scan(T.win[:, w + S6 + ST - 1:w + S6 - 1:-1], T.m6[:], T.win[:, w + ST - 1:end:-1], 0.0, A.mult, A.max))
 
-    def coarse(i, k_p):
-        w = i * WS
-        need("cv", k_mc, k_p)
+    def coarse(p, k_p):
+        b, n = p * RG, 2 * NB
+        need("cv", k_mc, k_mz, k_p)
         for m in range(1, 7):
-            mk = T.mc[:, 128 * (m - 1) + 1:128 * m]
-            ep = w + EX + 256 * m
-            es = ep + 128
-            done("cv", v.tensor_tensor_scan(T.win[:, ep + 1:ep + 128], T.win[:, w + P4 + 3:w + P4 + 508:4], mk, 0.0, A.max, A.mult))
-            tok = done("cv", v.tensor_tensor_scan(T.win[:, es + 126:es - 1:-1], T.win[:, w + P4 + 511:w + P4 + 3:-4], mk, 0.0, A.max, A.mult))
+            o = n * (m - 1)
+            done("cv", v.tensor_tensor_scan(T.win[:, b + EP + LV + m - 1:b + EP + 2 * ST:LV], T.win[:, b + P6 + B - 1:b + P6 + 2 * ST - B:B],
+                                            T.mc[:, o + 1:o + n], 0.0, A.max, A.mult))
+            tok = done("cv", v.tensor_tensor_scan(T.win[:, b + ES + LV * (n - 2) + m - 1:b + ES - 1:-LV], T.win[:, b + P6 + 2 * ST - 1:b + P6 + B:-B],
+                                                  T.mc[:, o + n - 1:o:-1], 0.0, A.max, A.mult))
         return tok
 
-    def tables(i):
-        k_p = prefix(i, 0, 0, 512)
-        suffix(i)
-        return coarse(i, k_p)
-
-    WIN = [(H0, P4), (H0, P4 + 512), (H0, S4), (0, S4)]
-    base = [CAPP * r[0] for r in halves(rank)] + [0]
+    WIN = [S6 + ST, P6 + ST, ES + ST, EP + ST]
 
     def part(i, e, c, n):
-        lo, hi = WIN[e]
-        o = e * NS + c // 16
-        return T.win[:, i * WS + lo:i * WS + hi].indirect(T.ou[:, o:o + n // 16])
+        o = (e % 2) * NS + c // 16
+        return T.win[:, at(i):at(i) + WIN[e]].indirect((T.oa if e < 2 else T.oc)[:, o:o + n // 16])
 
-    def gather(i, h, tab, lists=(0, 1, 2)):
-        need("cs_", k_ou, tab)
-        w, c, n = WORK[i, h], base[h], SL if h == 2 else HALF
-        for e in lists:
+    tok = {}
+
+    def gather(i, h, es, *deps):
+        w, (c, n) = WORK[i, h], CH[h]
+        for e in es:
             if e < w:
-                tok = done("cs_", s.activation(T["g%d%d" % (i, h)][:, e:w * n:w], part(i, e, c, n), F.Copy))
-        return tok
+                need("cs_", *deps)
+                tok[i, h] = done("cs_", s.activation(T["g%d%s" % (i, h)][:, e:w * n:w], part(i, e, c, n), F.Copy))
 
-    def best(i, h, tok):
-        w, c, n = WORK[i, h], base[h], SL if h == 2 else HALF
-        need("cv", k_m3 if w == 3 else k_m2, tok)
-        msk, src, dst = T.m3 if w == 3 else T.m2, T["g%d%d" % (i, h)], T["s%d%d" % (i, h)]
+    def best(i, h):
+        w, (c, n) = WORK[i, h], CH[h]
+        need("cv", k_ms[w], tok[i, h])
+        msk, src, dst = T["m%d" % w], T["g%d%s" % (i, h)], T["s%d%s" % (i, h)]
         k = done("cv", v.tensor_tensor_scan(dst[:, 0:w * n], msk[:, 0:w * n], src[:, 0:w * n], 0.0, A.mult, A.max))
         if w == 2:
             need("cv", k)
@@ -236,51 +282,58 @@ def rank_program(g, core, T, topo):
         return k
 
     def last(i, h, k):
-        w, c, n = WORK[i, h], base[h], SL if h == 2 else HALF
+        w, (c, n) = WORK[i, h], CH[h]
         need("cv", k)
-        cur = T["s%d%d" % (i, h)][:, 2:3 * n:3] if w == 3 else T["g%d%d" % (i, h)][:, 0:n]
+        cur = T["s%d%s" % (i, h)][:, 2:3 * n:3] if w == 3 else T["g%d%s" % (i, h)][:, 0:n]
         return done("cv", v.tensor_tensor(T.tile[:, 4 * c + i:4 * (c + n):4], part(i, 3, c, n), cur, A.max))
 
-    def pack(h, k):
-        c = base[h]
-        return quant(T.cq[:, c:c + HALF], T.cs[:, c:c + HALF], T.tile[:, 4 * c:4 * (c + HALF)], k)
+    def merge(*todo):
+        b = best(*todo[0])
+        for j, x in enumerate(todo):
+            n = best(*todo[j + 1]) if j + 1 < len(todo) else None
+            k = last(*x, b)
+            b = n
+        return k
 
-    prefix(0, 0, 0, XC)
-    need("cv", k_max)
-    k_ou = done("cv", v.tensor_copy(T.ou[:], T.of[:]))
-    kp = prefix(0, 1, XC, 512)
-    suffix(0)
+    def pack(c, n, k):
+        return quant(T.cq[:, c:c + n], T.cs[:, c:c + n], T.tile[:, 4 * c:4 * (c + n)], k)
+
+    prefix(0, 0, XC, k_h[0])
     k_a.append(quant(T.aq[:, 128:256], T.sa[:, 128:256], T.ab[:, 512:1024], ("a1", 16)))
     empty(1, product(1))
-    t0 = coarse(0, kp)
+    k_f = levels()
+    ks0 = suffix(0, k_h[4])
+    prefix(0, XC, ST)
+    k_oc = offsets(k_f)
     k_a.append(quant(T.aq[:, 256:512], T.sa[:, 256:512], T.ab[:, 1024:2048], ("a2", 16)))
     k_a.append(k_a[2])
     z2, z3 = product(2), product(3)
-    gather(0, 2, t0, (0,))
+    ks1 = suffix(1, k_h[1])
+    kp1 = prefix(1, 0, ST)
+    t01 = coarse(0, kp1)
+    gather(0, "a", (0,), k_oa, ks0, k_h[1])
+    gather(0, "a", (1,), ks1)
     empty(2, z2)
-    t1 = tables(1)
-    g0 = gather(0, 2, t0, (1, 2))
     empty(3, z3)
-    t2 = tables(2)
-    g1 = gather(1, 2, t1)
-    b0 = best(0, 2, g0)
-    kp = prefix(3, 0, 0, 512)
-    last(0, 2, b0)
-    suffix(3)
-    t3 = coarse(3, kp)
-    g20, g30 = gather(2, 0, t2), gather(3, 0, t3)
-    g21, g31 = gather(2, 1, t2), gather(3, 1, t3)
-    last(1, 2, best(1, 2, g1))
-    last(2, 0, best(2, 0, g20))
-    k_c0 = pack(0, last(3, 0, best(3, 0, g30)))
-    b21 = best(2, 1, g21)
-    b31 = best(3, 1, g31)
-    last(2, 1, b21)
-    k_c1 = pack(1, last(3, 1, b31))
+    gather(1, "f", (0, 1), kp1)
+    gather(0, "a", (2,), k_oc, t01)
+    gather(1, "f", (2,))
+    ks2, kp2 = suffix(2, k_h[2]), prefix(2, 0, ST)
+    ks3, kp3 = suffix(3, k_h[3]), prefix(3, 0, ST)
+    t23 = coarse(1, kp3)
+    gather(2, "f", (0, 1), ks3)
+    gather(3, "f", (0, 1), kp3)
+    for i, h in ((2, "f"), (3, "f")):
+        gather(i, h, (2,), t23)
+    for i, h in ((1, "n"), (2, "n"), (3, "n"), (0, "o"), (1, "o"), (2, "o"), (3, "o")):
+        gather(i, h, (0, 1, 2))
+    merge((0, "a"))
+    k_c0 = pack(0, FAR, merge((1, "f"), (2, "f"), (3, "f")))
+    k_c1 = pack(FAR, NEAR, merge((1, "n"), (2, "n"), (3, "n")))
 
     sent = 0
-    for h, (tok, half) in enumerate(zip((k_c0, k_c1), sending(rank, T, topo))):
-        need("cg", tok)
+    for h, (k, half) in enumerate(zip((k_c0, k_c1), sending(rank, T, topo))):
+        need("cg", k)
         for what in (0, 1):
             trs = []
             for r, es in half[what]:
@@ -288,7 +341,7 @@ def rank_program(g, core, T, topo):
                 msk = 0
                 for e in es:
                     msk |= 1 << e
-                a, b = CAPP * r, CAPP * places(r).index(rank)
+                a, b = CAPP * order(rank).index(r), CAPP * places(r).index(rank)
                 if what == 0:
                     src, out = T.cq[:, a:a + CAPP].bitcast(dt.uint8), T.rq[:, b:b + CAPP].bitcast(dt.uint8)
                 else:
@@ -305,46 +358,39 @@ def rank_program(g, core, T, topo):
 
     k_u = quant(T.uq[:], T.us[:], T.ub[:], ("uv", 32))
     k_v = quant(T.vq[:], T.vs[:], T.vb[:], ("uv", 32))
-    shift = [CAPP * (places(rank).index(q) - q) for q in range(N)]
-    steps = [(CAPP * q, shift[q - 1] - shift[q]) for q in range(1, N) if shift[q - 1] != shift[q]]
     need("cv", ("pfg", 256))
-    done("cv", v.tensor_scalar(T.pa[:], T.pl[:], shift[N - 1], None, A.add))
-    for j, (b, d) in enumerate(steps):
-        done("cv", v.tensor_scalar(T.pb[:, 32 * j:32 * j + 32], T.pl[:], b, d, A.is_lt, A.mult))
     k = done("cv", v.tensor_scalar(T.pz[:], T.pl[:, 16:32], 0, SL, A.is_lt, A.mult))
-    cur = T.pa
-    for j in range(len(steps)):
-        need("cv", k)
-        nxt = T.pc if cur is T.pa else T.pa
-        k = done("cv", v.tensor_tensor(nxt[:], cur[:], T.pb[:, 32 * j:32 * j + 32], A.add))
-        cur = nxt
+    merge((0, "o"))
     need("cv", k)
-    k = done("cv", v.tensor_tensor(cur[:, 16:32], cur[:, 16:32], T.pz[:], A.max))
+    k = done("cv", v.tensor_tensor(T.pl[:, 16:32], T.pl[:, 16:32], T.pz[:], A.max))
+    merge((1, "o"))
     need("cv", k)
-    k_pu = done("cv", v.tensor_copy(T.pu[:], cur[:]))
+    k_pu = done("cv", v.tensor_copy(T.pu[:], T.pl[:]))
+    k_co = quant(T.oq[:], T.ow[:], T.tile[:, 4 * (SL - 128):4 * SL], merge((2, "o"), (3, "o")))
 
-    ob = min(CAPP * rank, base[1] + HALF - 128)
-    oc = CAPP * rank - ob
-    ku = mm(T.pp[:, 0:HALF], T.uq[:], T.us[:], T.rq[:, 0:HALF], T.rs[:, 0:HALF], k_u, ("arr0", arrive[0]))
-    kv = mm(T.pp[:, 512:512 + HALF], T.vq[:], T.vs[:], T.rq[:, 0:HALF], T.rs[:, 0:HALF], k_v)
-    kuo = mm(T.pp[:, 1024:1152], T.uq[:], T.us[:], T.cq[:, ob:ob + 128], T.cs[:, ob:ob + 128], k_c1)
-    kvo = mm(T.pp[:, 1536:1664], T.vq[:], T.vs[:], T.cq[:, ob:ob + 128], T.cs[:, ob:ob + 128])
-    need("cs_", ku)
-    done("cs_", s.activation(T.zu[:, 0:HALF], T.pp[:, 0:HALF], F.Copy))
-    need("cs_", kuo)
-    k_uo = done("cs_", s.activation(T.zu[:, 320:384], T.pp[:, 1024 + oc:1024 + oc + CAPP], F.Copy))
-    need("cv", kv)
-    done("cv", v.tensor_copy(T.zv[:, 0:HALF], T.pp[:, 512:512 + HALF]))
-    need("cv", kvo)
-    k_vo = done("cv", v.tensor_copy(T.zv[:, 320:384], T.pp[:, 1536 + oc:1536 + oc + CAPP]))
+    ku = mm(T.pp[:, 0:FAR], T.uq[:], T.us[:], T.rq[:, 0:FAR], T.rs[:, 0:FAR], k_u, k_v, ("arr0", arrive[0]))
+    kv = mm(T.pp[:, 512:512 + FAR], T.vq[:], T.vs[:], T.rq[:, 0:FAR], T.rs[:, 0:FAR])
+    kuo = mm(T.pp[:, 1024:1152], T.uq[:], T.us[:], T.oq[:], T.ow[:], k_co)
+    kvo = mm(T.pp[:, 1536:1664], T.vq[:], T.vs[:], T.oq[:], T.ow[:])
 
-    ku = mm(T.zp[:, 0:128], T.uq[:], T.us[:], T.rq[:, HALF:320], T.rs[:, HALF:320], ("arr1", arrive[1]))
-    kv = mm(T.zp[:, 512:640], T.vq[:], T.vs[:], T.rq[:, HALF:320], T.rs[:, HALF:320])
-    need("cs_", ku)
-    k_zu2 = done("cs_", s.activation(T.zu[:, HALF:320], T.zp[:, 0:128], F.Copy))
-    need("cv", kv)
-    k_zv = done("cv", v.tensor_copy(T.zv[:, HALF:320], T.zp[:, 512:640]))
-    need("cs_", k_pu, k_zu2)
+    def natural(q, out, src, ranks, c, k):
+        need(q, k)
+        for o, r, n in runs(ranks):
+            d, x = out[:, CAPP * r:CAPP * (r + n)], src[:, c + CAPP * o:c + CAPP * (o + n)]
+            tok = done(q, s.activation(d, x, F.Copy) if q == "cs_" else v.tensor_copy(d, x))
+        return tok
+
+    far, near = places(rank)[0:3], places(rank)[3:5]
+    natural("cs_", T.zu, T.pp, far, 0, ku)
+    natural("cv", T.zv, T.pp, far, 512, kv)
+    natural("cs_", T.zu, T.pp, [rank], 1024 + 128 - CAPP, kuo)
+    natural("cv", T.zv, T.pp, [rank], 1536 + 128 - CAPP, kvo)
+
+    ku = mm(T.zp[:, 0:NEAR], T.uq[:], T.us[:], T.rq[:, FAR:320], T.rs[:, FAR:320], ("arr1", arrive[1]))
+    kv = mm(T.zp[:, 512:512 + NEAR], T.vq[:], T.vs[:], T.rq[:, FAR:320], T.rs[:, FAR:320])
+    k_zu2 = natural("cs_", T.zu, T.zp, near, 0, ku)
+    k_zv = natural("cv", T.zv, T.zp, near, 512, kv)
+    need("cs_", k_pu, k_zu, k_zu2)
     k_g = [done("cs_", s.activation(T.gu[:, 128 * h:128 * h + 128], T.zu[:].indirect(T.pu[:, 16 + 8 * h:24 + 8 * h]), F.Copy)) for h in (0, 1)]
     need("cv", k_zv)
     for h in (0, 1):

from concourse.bass import DstId, RemoteDMATransfer
from concourse.mybir import dt, AluOpType, ActivationFunctionType

N, T_COLS, CAPP, P = 6, 512, 64, 256
SL = N * CAPP
NS = SL // 16
CC = CAPP // 16
B = 6
ST = 528
NB = ST // B
LV = 6
XC = 43 * B
S6, P6 = 2 * ST, 4 * ST
W = 4768
CE, DE = -ST, -3 * ST
EP, ES = W + DE, W + CE
RG = ES + 2 * ST

FAR, NEAR = 3 * CAPP, 2 * CAPP
CH = {"a": (0, FAR + NEAR), "f": (0, FAR), "n": (FAR, NEAR), "o": (FAR + NEAR, CAPP)}
WORK = {(0, "a"): 3, (1, "f"): 3, (2, "f"): 3, (3, "f"): 3, (1, "n"): 3, (2, "n"): 3, (3, "n"): 3,
        (0, "o"): 3, (1, "o"): 3, (2, "o"): 3, (3, "o"): 3}

SCRATCH = {
    "xb": ("sbuf", [128, 2048], "bfloat16"), "ab": ("sbuf", [128, 2048], "bfloat16"),
    "ub": ("sbuf", [128, 512], "bfloat16"), "vb": ("sbuf", [128, 512], "bfloat16"),
    "xq": ("sbuf", [128, 512], "float8_e4m3fn_x4"), "xs": ("sbuf", [128, 512], "uint8"),
    "aq": ("sbuf", [128, 512], "float8_e4m3fn_x4"), "sa": ("sbuf", [128, 512], "uint8"),
    "uq": ("sbuf", [128, 128], "float8_e4m3fn_x4"), "us": ("sbuf", [128, 128], "uint8"),
    "vq": ("sbuf", [128, 128], "float8_e4m3fn_x4"), "vs": ("sbuf", [128, 128], "uint8"),
    "cq": ("sbuf", [128, 320], "float8_e4m3fn_x4"), "cs": ("sbuf", [128, 320], "uint8"),
    "oq": ("sbuf", [128, 128], "float8_e4m3fn_x4"), "ow": ("sbuf", [128, 128], "uint8"),
    "rq": ("sbuf", [128, 320], "float8_e4m3fn_x4"), "rs": ("sbuf", [128, 320], "uint8"),
    "win": ("sbuf", [128, 2 * RG], "bfloat16"),
    "tile": ("sbuf", [128, 4 * SL], "bfloat16"),
    "ones": ("sbuf", [128, 960], "bfloat16"), "m6": ("sbuf", [128, ST], "bfloat16"),
    "m3": ("sbuf", [128, 960], "bfloat16"), "m2": ("sbuf", [128, 640], "bfloat16"),
    "mc": ("sbuf", [128, 6 * 2 * NB], "bfloat16"), "aw": ("sbuf", [128, LV * NS], "bfloat16"),
    "ll": ("sbuf", [128, 2 * NS], "int32"), "lm": ("sbuf", [128, NS], "float32"),
    "ld": ("sbuf", [128, 4 * NS], "float32"), "l6": ("sbuf", [128, 2 * NS], "int32"), "sb": ("sbuf", [128, 2 * NS], "int32"),
    "sh": ("sbuf", [128, 2 * LV * NS], "int32"), "fl": ("sbuf", [128, LV * NS], "bfloat16"),
    "cn": ("sbuf", [128, LV * NS], "float32"), "ee": ("sbuf", [128, 2 * NS], "float32"),
    "yy": ("sbuf", [128, 2 * NS], "float32"), "xm": ("sbuf", [128, 2 * NS], "float32"),
    "dd": ("sbuf", [128, 2 * NS], "float32"), "fd": ("sbuf", [128, 2 * NS], "float32"),
    "of": ("sbuf", [128, 4 * NS], "float32"), "oa": ("sbuf", [128, 2 * NS], "uint16"), "oc": ("sbuf", [128, 2 * NS], "uint16"),
    "pl": ("sbuf", [128, 32], "int32"), "pz": ("sbuf", [128, 16], "int32"), "pu": ("sbuf", [128, 32], "uint16"),
    "zu": ("sbuf", [128, 400], "float32"), "zv": ("sbuf", [128, 384], "float32"),
    "gu": ("sbuf", [128, P], "float32"), "yb": ("sbuf", [128, P], "float32"),
    "zp": ("psum", [128, 2048], "float32"), "pp": ("psum", [128, 2048], "float32"),
}
for (_i, _h), _w in WORK.items():
    SCRATCH["g%d%s" % (_i, _h)] = ("sbuf", [128, _w * CH[_h][1]], "bfloat16")
    SCRATCH["s%d%s" % (_i, _h)] = ("sbuf", [128, _w * CH[_h][1]], "bfloat16")
SEMAPHORES = ["cv", "cs_", "ct", "cg", "lists", "x0", "x1", "a0", "a1", "a2", "uv", "pfg", "y0", "y1", "arr0", "arr1", "sent"]


def order(q):
    return [(q + 1 + k) % N for k in range(N)]


def places(r):
    return [(r + 3 + k) % N for k in range(3)] + [(r + 1 + k) % N for k in range(2)]


def runs(ranks):
    out = []
    for k, q in enumerate(ranks):
        if out and out[-1][1] + out[-1][2] == q:
            out[-1][2] += 1
        else:
            out.append([k, q, 1])
    return out


def sending(q, T, topo):
    out = []
    for ds in (order(q)[0:3], order(q)[3:5]):
        eng = topo.engines(T.cores[q], T.cores[ds[0]])
        ev, od = eng[0::2], eng[1::2]
        k = len(ev) // 2
        ds = sorted(ds, key=lambda r: topo.die(T.cores[r]) == topo.die(T.cores[q]))
        es = ([ev[:k], ev[k:], od], [od[:k], od[k:], ev]) if len(ds) == 3 else ([ev, od], [od, ev])
        out.append([[(r, e) for r, e in zip(ds, x)] for x in es])
    return out


def rank_program(g, core, T, topo):
    rank = T.rank_of(core)
    if rank is None:
        return
    A, F = AluOpType, ActivationFunctionType
    que = {"cv": g.vector, "cs_": g.scalar, "ct": g.tensor, "cg": g, "sy": g.sync}
    count = {k: 0 for k in que}
    seen = {k: {} for k in que}
    v, s, t = g.vector, g.scalar, g.tensor

    def need(q, *toks):
        for sem, val in toks:
            if seen[q].get(sem, 0) < val:
                que[q].wait_ge(T.sem[sem], val)
                seen[q][sem] = val

    def done(q, ins):
        ins.then_inc(T.sem[q], 1)
        count[q] += 1
        return (q, count[q])

    s.dma_start(T.ll[:, NS:2 * NS], T.ln[:]).then_inc(T.sem.lists, 16)
    g.sync.dma_start(T.ll[:, 0:NS], T.lo[:]).then_inc(T.sem.lists, 16)
    g.sync.dma_start(T.xb[:, 0:4 * XC], T.x[:, 0:4 * XC]).then_inc(T.sem.x0, 16)
    s.dma_start(T.ab[:, 0:512], T.a[:, 0:512]).then_inc(T.sem.a0, 16)
    g.sync.dma_start(T.xb[:, 4 * XC:2048], T.x[:, 4 * XC:2048]).then_inc(T.sem.x1, 16)
    g.sync.dma_start(T.ab[:, 512:1024], T.a[:, 512:1024]).then_inc(T.sem.a1, 16)
    g.sync.dma_start(T.ab[:, 1024:2048], T.a[:, 1024:2048]).then_inc(T.sem.a2, 16)
    g.sync.dma_start(T.ub[:], T.u[:]).then_inc(T.sem.uv, 16)
    g.sync.dma_start(T.vb[:], T.v[:]).then_inc(T.sem.uv, 16)
    for k in range(8):
        g.sync.dma_start(T.pl[16 * k:16 * k + 16, 0:16], T.pf[:]).then_inc(T.sem.pfg, 16)
        g.sync.dma_start(T.pl[16 * k:16 * k + 16, 16:32], T.pg[:]).then_inc(T.sem.pfg, 16)

    k_one = done("cv", v.memset(T.ones[:], 1.0))
    k_mo = done("cv", v.memset(T.mc[:, 3 * 2 * NB:6 * 2 * NB], 1.0))
    k_aw = done("cv", v.memset(T.aw[:], 1.0))
    k_zu = done("cv", v.memset(T.zu[:, 384:400], 0.0))
    need("cv", k_aw)
    done("cv", v.memset(T.aw[:, 0::LV], 0.0))
    k_aw = done("cv", v.memset(T.aw[:, 1::LV], float(W)))

    need("cg", k_one)

    def mask(out, n, b):
        return done("cg", g.affine_select(out, T.ones[:, 0:n], [[0, n // b], [1, b]], A.is_gt, 0.0, 0, 0))

    k_m6 = mask(T.m6[:], ST, B)
    for m in range(1, 4):
        k_mc = mask(T.mc[:, 2 * NB * (m - 1):2 * NB * m], 2 * NB, 1 << m)
    k_ms = {3: mask(T.m3[:], 960, 3)}
    if 2 in WORK.values():
        k_ms[2] = mask(T.m2[:], 640, 2)

    def zero(out, n):
        return done("cs_", s.activation(out, T.ones[:, 0:n], F.Copy, scale=0.0))

    need("cs_", k_one)
    for i in range(4):
        b = (i // 2) * RG + (i % 2) * ST
        k_hp = zero(T.win[:, b + T_COLS:b + ST], ST - T_COLS)
    for p in range(2):
        zero(T.win[:, p * RG + 6 * ST:p * RG + EP + LV], EP + LV - 6 * ST)
        zero(T.win[:, p * RG + ES + 2 * ST - LV:p * RG + RG], LV)
    need("cs_", k_mo)
    for m in range(4, 7):
        for p in range(2):
            b = 2 * NB * (m - 1) + NB * p
            k_mz = zero(T.mc[:, b:b + NB:1 << m], len(range(0, NB, 1 << m)))

    c = CC * ((rank + 1) % N)
    cuts = [(0, c, NS - c)] + ([(NS - c, 0, c)] if c else [])
    need("cv", ("lists", 32))
    for o, b, n in cuts:
        done("cv", v.tensor_copy(T.ld[:, NS + o:NS + o + n], T.ll[:, b:b + n]))
    for o, b, n in cuts:
        k_lm = done("cv", v.tensor_scalar(T.lm[:, o:o + n], T.ll[:, NS + b:NS + b + n], -1, None, A.add))
    LR = T.ld[:, NS:3 * NS]
    need("cv", k_lm)
    k = done("cv", v.tensor_tensor(T.ld[:, 2 * NS:3 * NS], T.ld[:, NS:2 * NS], T.lm[:], A.add))
    need("cv", k)
    k = done("cv", v.tensor_scalar(T.l6[:], LR, 171, None, A.mult))
    need("cs_", k_lm)
    done("cs_", s.activation(T.ee[:, 0:NS], T.lm[:], F.Sign))
    k_ee = done("cs_", s.activation(T.ee[:, NS:2 * NS], T.lm[:], F.Sign, scale=-1.0))
    need("cv", k)
    k = done("cv", v.tensor_scalar(T.sb[:], T.l6[:], 10, None, A.arith_shift_right))
    for j in range(3):
        done("cv", v.tensor_scalar(T.sh[:, j::LV], T.l6[:], 11 + j, None, A.arith_shift_right))
    need("cv", k)
    done("cv", v.tensor_scalar(T.ld[:, 0:NS], T.sb[:, 0:NS], B, CE, A.mult, A.add))
    k_ld = done("cv", v.tensor_scalar(T.ld[:, 3 * NS:4 * NS], T.sb[:, NS:2 * NS], B, DE, A.mult, A.add))

    def quant(out, sc, src, *deps):
        need("cv", *deps)
        return done("cv", v.quantize_mx(out, sc, src))

    k_x0 = quant(T.xq[:, 0:XC], T.xs[:, 0:XC], T.xb[:, 0:4 * XC], ("x0", 16))
    need("cv", k_ld)
    k = done("cv", v.tensor_tensor(T.dd[:], T.ld[:, 0:2 * NS], T.ld[:, 2 * NS:4 * NS], A.subtract))
    k_a = [quant(T.aq[:, 0:128], T.sa[:, 0:128], T.ab[:, 0:512], ("a0", 16))]
    need("cv", k)
    done("cv", v.tensor_scalar(T.fd[:, 0:NS], T.dd[:, 0:NS], CE - (B - 1), S6, A.is_le, A.mult))
    k = done("cv", v.tensor_scalar(T.fd[:, NS:2 * NS], T.dd[:, NS:2 * NS], -DE, P6, A.is_le, A.mult))
    for j in range(3, LV):
        k_sh = done("cv", v.tensor_scalar(T.sh[:, j::LV], T.l6[:], 11 + j, None, A.arith_shift_right))
    need("cv", k)
    k = done("cv", v.tensor_tensor(T.of[:, 0:2 * NS], LR, T.fd[:], A.add))
    k_x1 = quant(T.xq[:, XC:512], T.xs[:, XC:512], T.xb[:, 4 * XC:2048], ("x1", 16))
    need("cv", k)
    k_oa = done("cv", v.tensor_copy(T.oa[:], T.of[:, 0:2 * NS]))

    def levels():
        need("cv", k_sh)
        return done("cv", v.tensor_tensor(T.fl[:], T.sh[:, 0:LV * NS], T.sh[:, LV * NS:2 * LV * NS], A.not_equal))

    def offsets(k):
        need("cv", k, k_aw)
        k = done("cv", v.tensor_tensor_scan(T.cn[:], T.aw[:], T.fl[:], 0.0, A.mult, A.add))
        need("cv", k_ee)
        done("cv", v.tensor_tensor(T.yy[:], LR, T.ee[:], A.add))
        need("cv", k)
        done("cv", v.tensor_tensor(T.xm[:, 0:NS], T.ld[:, 0:NS], T.cn[:, LV - 1::LV], A.add))
        k = done("cv", v.tensor_tensor(T.xm[:, NS:2 * NS], T.ld[:, 3 * NS:4 * NS], T.cn[:, LV - 1::LV], A.add))
        need("cv", k)
        k = done("cv", v.tensor_tensor(T.of[:, 2 * NS:4 * NS], T.xm[:], T.yy[:], A.max))
        need("cv", k)
        return done("cv", v.tensor_copy(T.oc[:], T.of[:, 2 * NS:4 * NS]))

    def mm(out, w, ws, x, xs, *deps):
        need("ct", *deps)
        return done("ct", t.matmul_mx(out, w, ws, x, xs, True, True))

    def at(i):
        return (i // 2) * RG + (i % 2) * ST

    def relu(i, c, n, src, *deps):
        need("cs_", *deps)
        return done("cs_", s.activation(T.win[:, at(i) + c:at(i) + c + n], src, F.Relu, scale=0.05))

    k0 = mm(T.zp[:, 0:XC], T.aq[:, 0:128], T.sa[:, 0:128], T.xq[:, 0:XC], T.xs[:, 0:XC], k_x0, k_a[0])
    k1 = mm(T.pp[:, 1536:2048 - XC], T.aq[:, 0:128], T.sa[:, 0:128], T.xq[:, XC:512], T.xs[:, XC:512], k_x1)
    k_h = {0: relu(0, 0, XC, T.zp[:, 0:XC], k0), 4: relu(0, XC, 512 - XC, T.pp[:, 1536:2048 - XC], k1)}

    def product(i):
        return mm(T.zp[:, 512 * i:512 * i + 512], T.aq[:, 128 * i:128 * i + 128], T.sa[:, 128 * i:128 * i + 128], T.xq[:], T.xs[:], k_a[i])

    def empty(i, k):
        k_h[i] = relu(i, 0, 512, T.zp[:, 512 * i:512 * i + 512], k)

    def prefix(i, a, b, *deps):
        w = at(i)
        need("cv", k_m6, k_hp, *deps)
        return done("cv", v.tensor_tensor_scan(T.win[:, w + P6 + a:w + P6 + b], T.m6[:, a:b], T.win[:, w + a:w + b], 0.0, A.mult, A.max))

    def suffix(i, *deps):
        w = at(i)
        need("cv", k_m6, k_hp, *deps)
        end = w - 1 if w else None
        return done("cv", v.tensor_tensor_scan(T.win[:, w + S6 + ST - 1:w + S6 - 1:-1], T.m6[:], T.win[:, w + ST - 1:end:-1], 0.0, A.mult, A.max))

    def coarse(p, k_p):
        b, n = p * RG, 2 * NB
        need("cv", k_mc, k_mz, k_p)
        for m in range(1, 7):
            o = n * (m - 1)
            done("cv", v.tensor_tensor_scan(T.win[:, b + EP + LV + m - 1:b + EP + 2 * ST:LV], T.win[:, b + P6 + B - 1:b + P6 + 2 * ST - B:B],
                                            T.mc[:, o + 1:o + n], 0.0, A.max, A.mult))
            tok = done("cv", v.tensor_tensor_scan(T.win[:, b + ES + LV * (n - 2) + m - 1:b + ES - 1:-LV], T.win[:, b + P6 + 2 * ST - 1:b + P6 + B:-B],
                                                  T.mc[:, o + n - 1:o:-1], 0.0, A.max, A.mult))
        return tok

    WIN = [S6 + ST, P6 + ST, ES + ST, EP + ST]

    def part(i, e, c, n):
        o = (e % 2) * NS + c // 16
        return T.win[:, at(i):at(i) + WIN[e]].indirect((T.oa if e < 2 else T.oc)[:, o:o + n // 16])

    tok = {}

    def gather(i, h, es, *deps):
        w, (c, n) = WORK[i, h], CH[h]
        for e in es:
            if e < w:
                need("cs_", *deps)
                tok[i, h] = done("cs_", s.activation(T["g%d%s" % (i, h)][:, e:w * n:w], part(i, e, c, n), F.Copy))

    def best(i, h):
        w, (c, n) = WORK[i, h], CH[h]
        need("cv", k_ms[w], tok[i, h])
        msk, src, dst = T["m%d" % w], T["g%d%s" % (i, h)], T["s%d%s" % (i, h)]
        k = done("cv", v.tensor_tensor_scan(dst[:, 0:w * n], msk[:, 0:w * n], src[:, 0:w * n], 0.0, A.mult, A.max))
        if w == 2:
            need("cv", k)
            k = done("cv", v.tensor_tensor(src[:, 0:n], part(i, 2, c, n), dst[:, 1:2 * n:2], A.max))
        return k

    def last(i, h, k):
        w, (c, n) = WORK[i, h], CH[h]
        need("cv", k)
        cur = T["s%d%s" % (i, h)][:, 2:3 * n:3] if w == 3 else T["g%d%s" % (i, h)][:, 0:n]
        return done("cv", v.tensor_tensor(T.tile[:, 4 * c + i:4 * (c + n):4], part(i, 3, c, n), cur, A.max))

    def merge(*todo):
        b = best(*todo[0])
        for j, x in enumerate(todo):
            n = best(*todo[j + 1]) if j + 1 < len(todo) else None
            k = last(*x, b)
            b = n
        return k

    def pack(c, n, k):
        return quant(T.cq[:, c:c + n], T.cs[:, c:c + n], T.tile[:, 4 * c:4 * (c + n)], k)

    prefix(0, 0, XC, k_h[0])
    k_a.append(quant(T.aq[:, 128:256], T.sa[:, 128:256], T.ab[:, 512:1024], ("a1", 16)))
    empty(1, product(1))
    k_f = levels()
    ks0 = suffix(0, k_h[4])
    prefix(0, XC, ST)
    k_oc = offsets(k_f)
    k_a.append(quant(T.aq[:, 256:512], T.sa[:, 256:512], T.ab[:, 1024:2048], ("a2", 16)))
    k_a.append(k_a[2])
    z2, z3 = product(2), product(3)
    ks1 = suffix(1, k_h[1])
    kp1 = prefix(1, 0, ST)
    t01 = coarse(0, kp1)
    gather(0, "a", (0,), k_oa, ks0, k_h[1])
    gather(0, "a", (1,), ks1)
    empty(2, z2)
    empty(3, z3)
    gather(1, "f", (0, 1), kp1)
    gather(0, "a", (2,), k_oc, t01)
    gather(1, "f", (2,))
    ks2, kp2 = suffix(2, k_h[2]), prefix(2, 0, ST)
    ks3, kp3 = suffix(3, k_h[3]), prefix(3, 0, ST)
    t23 = coarse(1, kp3)
    gather(2, "f", (0, 1), ks3)
    gather(3, "f", (0, 1), kp3)
    for i, h in ((2, "f"), (3, "f")):
        gather(i, h, (2,), t23)
    for i, h in ((1, "n"), (2, "n"), (3, "n"), (0, "o"), (1, "o"), (2, "o"), (3, "o")):
        gather(i, h, (0, 1, 2))
    merge((0, "a"))
    k_c0 = pack(0, FAR, merge((1, "f"), (2, "f"), (3, "f")))
    k_c1 = pack(FAR, NEAR, merge((1, "n"), (2, "n"), (3, "n")))

    sent = 0
    for h, (k, half) in enumerate(zip((k_c0, k_c1), sending(rank, T, topo))):
        need("cg", k)
        for what in (0, 1):
            trs = []
            for r, es in half[what]:
                rid, pnc = topo.addr(T.cores[r])[0:2]
                msk = 0
                for e in es:
                    msk |= 1 << e
                a, b = CAPP * order(rank).index(r), CAPP * places(r).index(rank)
                if what == 0:
                    src, out = T.cq[:, a:a + CAPP].bitcast(dt.uint8), T.rq[:, b:b + CAPP].bitcast(dt.uint8)
                else:
                    src, out = T.cs[:, a:a + CAPP], T.rs[:, b:b + CAPP]
                trs.append(RemoteDMATransfer(dst_ids=[DstId(rid=rid, pnc=pnc)], dma_engine_mask=msk, remote_sem=T.sem["arr%d" % h], src=src, dst=out))
                sent += len(es)
            g.remote_dma_fused(trs, local_sem=T.sem.sent)
    arrive = [0, 0]
    for q in range(N):
        if q != rank:
            for h, half in enumerate(sending(q, T, topo)):
                for what in half:
                    arrive[h] += sum(len(es) for r, es in what if r == rank)

    k_u = quant(T.uq[:], T.us[:], T.ub[:], ("uv", 32))
    k_v = quant(T.vq[:], T.vs[:], T.vb[:], ("uv", 32))
    need("cv", ("pfg", 256))
    k = done("cv", v.tensor_scalar(T.pz[:], T.pl[:, 16:32], 0, SL, A.is_lt, A.mult))
    merge((0, "o"))
    need("cv", k)
    k = done("cv", v.tensor_tensor(T.pl[:, 16:32], T.pl[:, 16:32], T.pz[:], A.max))
    merge((1, "o"))
    need("cv", k)
    k_pu = done("cv", v.tensor_copy(T.pu[:], T.pl[:]))
    k_co = quant(T.oq[:], T.ow[:], T.tile[:, 4 * (SL - 128):4 * SL], merge((2, "o"), (3, "o")))

    ku = mm(T.pp[:, 0:FAR], T.uq[:], T.us[:], T.rq[:, 0:FAR], T.rs[:, 0:FAR], k_u, k_v, ("arr0", arrive[0]))
    kv = mm(T.pp[:, 512:512 + FAR], T.vq[:], T.vs[:], T.rq[:, 0:FAR], T.rs[:, 0:FAR])
    kuo = mm(T.pp[:, 1024:1152], T.uq[:], T.us[:], T.oq[:], T.ow[:], k_co)
    kvo = mm(T.pp[:, 1536:1664], T.vq[:], T.vs[:], T.oq[:], T.ow[:])

    def natural(q, out, src, ranks, c, k):
        need(q, k)
        for o, r, n in runs(ranks):
            d, x = out[:, CAPP * r:CAPP * (r + n)], src[:, c + CAPP * o:c + CAPP * (o + n)]
            tok = done(q, s.activation(d, x, F.Copy) if q == "cs_" else v.tensor_copy(d, x))
        return tok

    far, near = places(rank)[0:3], places(rank)[3:5]
    natural("cs_", T.zu, T.pp, far, 0, ku)
    natural("cv", T.zv, T.pp, far, 512, kv)
    natural("cs_", T.zu, T.pp, [rank], 1024 + 128 - CAPP, kuo)
    natural("cv", T.zv, T.pp, [rank], 1536 + 128 - CAPP, kvo)

    ku = mm(T.zp[:, 0:NEAR], T.uq[:], T.us[:], T.rq[:, FAR:320], T.rs[:, FAR:320], ("arr1", arrive[1]))
    kv = mm(T.zp[:, 512:512 + NEAR], T.vq[:], T.vs[:], T.rq[:, FAR:320], T.rs[:, FAR:320])
    k_zu2 = natural("cs_", T.zu, T.zp, near, 0, ku)
    k_zv = natural("cv", T.zv, T.zp, near, 512, kv)
    need("cs_", k_pu, k_zu, k_zu2)
    k_g = [done("cs_", s.activation(T.gu[:, 128 * h:128 * h + 128], T.zu[:].indirect(T.pu[:, 16 + 8 * h:24 + 8 * h]), F.Copy)) for h in (0, 1)]
    need("cv", k_zv)
    for h in (0, 1):
        need("cv", k_g[h])
        k = done("cv", v.tensor_tensor(T.yb[:, 128 * h:128 * h + 128], T.zv[:].indirect(T.pu[:, 8 * h:8 * h + 8]), T.gu[:, 128 * h:128 * h + 128], A.add))
        need("sy", k)
        g.sync.dma_start(T.y[:, 128 * h:128 * h + 128], T.yb[:, 128 * h:128 * h + 128]).then_inc(T.sem["y%d" % h], 16)
    g.wait_ge(T.sem.sent, sent)
    need("sy", ("cs_", count["cs_"]), ("ct", count["ct"]), ("cg", count["cg"]), ("y0", 16), ("y1", 16))
